import numpy as np
import ml_dtypes


def mxq(x, axis, fmt="e4m3"):
    dtype, down = {"e4m3": (ml_dtypes.float8_e4m3fn, 7), "e5m2": (ml_dtypes.float8_e5m2, 14)}[fmt]
    v = np.moveaxis(np.asarray(x, np.float32).astype(ml_dtypes.bfloat16).astype(np.float64), axis, -1)
    blocks = v.reshape(v.shape[:-1] + (-1, 32))
    amax = np.abs(blocks).max(-1, keepdims=True)
    byte = np.maximum(np.where(amax > 0, np.frexp(amax)[1] - 1 + 127, 0) - down, 1)
    scale = np.exp2(byte - 127.0)
    codes = (blocks / scale).astype(np.float32).astype(dtype).astype(np.float64)
    return np.moveaxis((codes * scale).reshape(v.shape), -1, axis)


WIDE = False


def mx_kscale(k):
    if not WIDE:
        return np.ones(k)
    levels = np.array([10, -10, 5, -5, 0])
    if k % 512:
        return np.exp2(np.random.permutation(np.resize(levels, k // 32))).repeat(32)
    a = np.empty((k // 512, 16))
    for p in range(k // 512):
        a[p, :8] = np.random.permutation(np.resize(levels, 8))
        for g in range(8):
            far = levels[np.abs(levels - a[p, g]) >= 10]
            a[p, g + 8] = far[np.random.randint(len(far))]
    return np.exp2(a.ravel()).repeat(32)


def f64(x):
    return np.asarray(x).astype(np.float64)


def striped(idx):
    return np.tile(idx.reshape(-1, 16).T, (8, 1)).astype(np.uint16)


def unstriped(offs):
    return offs[:16].T.reshape(-1).astype(np.int64)


def striped8(idx):
    return np.concatenate([x.reshape(-1, 16).T for x in idx]).astype(np.uint16)


def runs(offs, k):
    lists = np.stack([offs[16 * r : 16 * r + 16].T.reshape(-1) for r in range(8)]).astype(np.int64)
    return lists[np.arange(k) % 512 // 64]


def pack_weight(w):
    k, n = w.shape
    w = f64(np.asarray(w, np.float32).astype(ml_dtypes.bfloat16)).reshape(k // 32, 32, n)
    amax = np.abs(w).max(1)
    byte = np.clip(np.where(amax > 0, np.frexp(amax)[1] - 1 + 127 - 7, 1), 1, 254)
    scaled = (w * np.exp2(127.0 - byte)[:, None, :]).reshape(k, n).astype(np.float32)
    words = np.ascontiguousarray(scaled.reshape(k // 512, 128, 4, n).transpose(0, 1, 3, 2)).astype(ml_dtypes.float8_e4m3fn).view(np.uint8)
    return words, np.ascontiguousarray(byte.astype(np.uint8).reshape(k // 512, 16, n))


def unpack_weight(words, scales):
    g, p, n, _ = words.shape
    vals = np.ascontiguousarray(words).view(ml_dtypes.float8_e4m3fn).astype(np.float64) * np.repeat(np.exp2(scales.astype(np.float64) - 127.0), 8, axis=1)[..., None]
    return vals.transpose(0, 1, 3, 2).reshape(g * 512, n)


def relu(v):
    return np.maximum(v, 0.0)


K, T, S, N, H, U = 1024, 2048, 512, 512, 512, 512


def setup_inputs():
    n = np.random.standard_normal
    s = mx_kscale(K)[:, None]
    u = mx_kscale(H)
    packed_xT = pack_weight(n((K, T)) * s)
    return {
        "x_words": packed_xT[0],
        "x_scales": packed_xT[1],
        "w1": (n((K, H)) / np.sqrt(K) / s * u).astype(np.float32),
        "slope": np.random.uniform(-0.5, 0.5, (H, U)).astype(np.float32),
        "w2": (n((H, N)) / np.sqrt(H) / u[:, None]).astype(np.float32),
        "offs": striped(np.random.permutation(T)[:S]),
        "task": striped8(np.stack([np.random.permutation(U)[(U * np.random.uniform(0, 1, S) ** 4).astype(np.int64)] for _ in range(8)])),
    }


def reference(x_words, x_scales, w1, slope, w2, offs, task):
    xq = unpack_weight(x_words, x_scales)[:, unstriped(offs)]
    y = mxq(f64(w1), 0, "e4m3").T @ xq
    q = relu(y)
    z = q + (y - q) * (f64(slope)[np.arange(H)[:, None], runs(task, H)])
    return mxq(f64(w2), 0, "e4m3").T @ mxq(z, 0, "e4m3")

@@ -1,0 +1,203 @@
+from contextlib import ExitStack
+
+import concourse.mybir as mybir
+
+K, T, S, N, H, U = 1024, 2048, 512, 512, 512, 512
+FLOPS = 2 * K * H * S + 2 * H * N * S
+
+F32 = mybir.dt.float32
+BF16 = mybir.dt.bfloat16
+I32 = mybir.dt.int32
+U32 = mybir.dt.uint32
+U16 = mybir.dt.uint16
+U8 = mybir.dt.uint8
+FP8X4 = mybir.dt.float8_e4m3fn_x4
+ALU = mybir.AluOpType
+RELU = mybir.ActivationFunctionType.Relu
+
+P = 128
+PACK = 4
+PASSES = K // (P * PACK)
+HALF = S // 2
+CHUNK = 128
+CHUNKS = S // CHUNK
+M_TILES = N // P
+
+
+def tile_picked_prelu8_none_p_kernel(tc, x_words, x_scales, w1, slope, w2, offs, task, out):
+    nc = tc.nc
+    with ExitStack() as ctx:
+        keep = ctx.enter_context(tc.tile_pool(name="keep", bufs=1))
+        psum_y = ctx.enter_context(tc.psum_pool(name="psum_y", bufs=4))
+        psum_o = ctx.enter_context(tc.psum_pool(name="psum_o", bufs=4))
+
+        def sb(name, shape, dtype):
+            return keep.tile(shape, dtype, name=name, align_bytes=64)
+
+        task_list = sb("task_list", [P, S // 16], U16)
+        offs_list = sb("offs_list", [P, S // 16], U16)
+        slope_rows = [sb(f"slope_rows{t}", [P, U], F32) for t in range(PACK)]
+        w1_raw = [sb(f"w1_raw{g}", [P, PACK, H], F32) for g in range(PASSES)]
+        w2_raw = [sb(f"w2_raw{h}", [P, PACK, N // 2], F32) for h in range(2)]
+        x_table = [sb(f"x_table{g}", [P, T], I32) for g in range(PASSES)]
+        x_scale_table = sb("x_scale_table", [P, T], U8)
+
+        nc.vector.memset(x_scale_table[:].bitcast(I32), 0)
+
+        nc.sync.dma_start(task_list[:], task)
+        slope_view = slope.rearrange("(p t) u -> p t u", t=PACK)
+        for t in range(PACK):
+            nc.sync.dma_start(slope_rows[t][:], slope_view[:, t, :])
+        w1_view = w1.rearrange("(g p j) c -> g p j c", p=P, j=PACK)
+        for g in range(PASSES):
+            nc.sync.dma_start(w1_raw[g][:], w1_view[g])
+        nc.sync.dma_start(offs_list[:], offs)
+        for q in range(4):
+            nc.scalar.dma_start(
+                x_scale_table[32 * q : 32 * q + 4 * PASSES, :].bitcast(I32),
+                x_scales[:, 4 * q : 4 * q + 4, :].bitcast(I32),
+            )
+        for g in range(PASSES):
+            nc.sync.dma_start(x_table[g][:], x_words[g].rearrange("p n t -> p (n t)").bitcast(I32))
+        w2_view = w2.rearrange("(p j) c -> p j c", j=PACK)
+        for h in range(2):
+            nc.sync.dma_start(w2_raw[h][:], w2_view[:, :, h * (N // 2) : (h + 1) * (N // 2)])
+
+        picked_slope = [sb(f"picked_slope{h}", [P, PACK, HALF], F32) for h in range(2)]
+        for t in range(PACK):
+            for h in range(2):
+                nc.vector.tensor_copy(
+                    picked_slope[h][:, t, :],
+                    slope_rows[t][:].indirect(task_list[:, h * HALF // 16 : (h + 1) * HALF // 16]),
+                )
+
+        w1_codes = [sb(f"w1_codes{g}", [P, H], U32) for g in range(PASSES)]
+        w1_scales = [sb(f"w1_scales{g}", [P, H], U8) for g in range(PASSES)]
+        w1_bf = [sb(f"w1_bf{g}", [P, H * PACK], BF16) for g in range(PASSES)]
+        for g in range(PASSES):
+            nc.scalar.copy(
+                w1_bf[g][:].rearrange("p (t m j) -> p m j t", t=PACK, j=PACK),
+                w1_raw[g][:].rearrange("p j (m t) -> p m j t", t=PACK),
+            )
+        x_picked_scales = sb("x_picked_scales", [P, S], U8)
+        x_first = sb("x_first", [P, S], U32)
+        x_second = [sb(f"x_second{h}", [P, HALF], U32) for h in range(2)]
+        nc.vector.quantize_mx(out=w1_codes[0][:].bitcast(FP8X4), scales=w1_scales[0][:], in_=w1_bf[0][:])
+        nc.vector.tensor_copy(x_picked_scales[:], x_scale_table[:].indirect(offs_list[:]))
+        nc.vector.tensor_copy(x_first[:], x_table[0][:].bitcast(U32).indirect(offs_list[:]))
+        nc.vector.quantize_mx(out=w1_codes[1][:].bitcast(FP8X4), scales=w1_scales[1][:], in_=w1_bf[1][:])
+        for h in range(2):
+            nc.vector.tensor_copy(
+                x_second[h][:],
+                x_table[1][:].bitcast(U32).indirect(offs_list[:, h * HALF // 16 : (h + 1) * HALF // 16]),
+            )
+
+        w2_codes = sb("w2_codes", [P, N], U32)
+        w2_scales = sb("w2_scales", [P, N], U8)
+        w2_bf = [sb(f"w2_bf{h}", [P, N // 2 * PACK], BF16) for h in range(2)]
+
+        def round_w2(h):
+            nc.scalar.copy(
+                w2_bf[h][:].rearrange("p (c i j) -> p c j i", i=4, j=PACK),
+                w2_raw[h][:].rearrange("p j (c i) -> p c j i", i=4),
+            )
+
+        def quantize_w2(h):
+            cols = slice(h * (N // 2), (h + 1) * (N // 2))
+            nc.vector.quantize_mx(out=w2_codes[:, cols].bitcast(FP8X4), scales=w2_scales[:, cols], in_=w2_bf[h][:])
+
+        y = [psum_y.tile([P, PACK, CHUNK], F32, name="y") for c in range(CHUNKS)]
+        below = [sb(f"below{c}", [P, CHUNK, PACK], BF16) for c in range(CHUNKS)]
+        above = [sb(f"above{c}", [P, CHUNK, PACK], BF16) for c in range(CHUNKS)]
+        z_bf = [sb(f"z_bf{c}", [P, CHUNK * PACK], BF16) for c in range(CHUNKS)]
+        z_codes = [sb(f"z_codes{c}", [P, CHUNK], U32) for c in range(CHUNKS)]
+        z_scales = [sb(f"z_scales{c}", [P, CHUNK], U8) for c in range(CHUNKS)]
+        out_view = out.rearrange("(i p) s -> p i s", p=P)
+
+        def first_product_pass(c, t, g):
+            cols = slice(c * CHUNK, (c + 1) * CHUNK)
+            in_half = slice(c % 2 * CHUNK, (c % 2 + 1) * CHUNK)
+            moving = [x_first[:, cols], x_second[c // 2][:, in_half]]
+            nc.tensor.matmul_mx(
+                out=y[c][:, t, :],
+                lhsT=w1_codes[g][:, t * P : (t + 1) * P].bitcast(FP8X4),
+                lhsT_scale=w1_scales[g][:, t * P : (t + 1) * P],
+                rhs=moving[g].bitcast(FP8X4),
+                rhs_scale=x_picked_scales[4 * g : P, cols],
+                start=(g == 0),
+                stop=(g == PASSES - 1),
+            )
+
+        def negative_part(c):
+            in_half = slice(c % 2 * CHUNK, (c % 2 + 1) * CHUNK)
+            nc.vector.scalar_tensor_tensor(
+                out=below[c][:],
+                in0=y[c][:].rearrange("p t s -> p s t"),
+                scalar=0.0,
+                in1=picked_slope[c // 2][:, :, in_half].rearrange("p t s -> p s t"),
+                op0=ALU.min,
+                op1=ALU.mult,
+            )
+
+        def positive_part(c):
+            nc.scalar.activation(out=above[c][:], in_=y[c][:].rearrange("p t s -> p s t"), func=RELU)
+
+        def join(c):
+            nc.vector.tensor_tensor(
+                z_bf[c][:],
+                below[c][:].rearrange("p s t -> p (s t)"),
+                above[c][:].rearrange("p s t -> p (s t)"),
+                ALU.add,
+            )
+
+        def quantize_z(c):
+            nc.vector.quantize_mx(out=z_codes[c][:].bitcast(FP8X4), scales=z_scales[c][:], in_=z_bf[c][:])
+
+        def second_product(c, tiles, copy, queue):
+            acc = psum_o.tile([P, len(tiles), CHUNK], F32, name="acc")
+            for n, i in enumerate(tiles):
+                nc.tensor.matmul_mx(
+                    out=acc[:, n, :],
+                    lhsT=w2_codes[:, i * P : (i + 1) * P].bitcast(FP8X4),
+                    lhsT_scale=w2_scales[:, i * P : (i + 1) * P],
+                    rhs=z_codes[c][:].bitcast(FP8X4),
+                    rhs_scale=z_scales[c][:],
+                    start=True,
+                    stop=True,
+                )
+            result = sb(f"result{c}_{tiles[0]}", [P, len(tiles), CHUNK], F32)
+            copy(result[:], acc[:])
+            queue.dma_start(out_view[:, tiles[0] : tiles[-1] + 1, c * CHUNK : (c + 1) * CHUNK], result[:])
+
+        for c in range(CHUNKS):
+            first_product_pass(c, 0, 0)
+        for c in range(CHUNKS):
+            first_product_pass(c, 0, 1)
+            for t in range(1, PACK):
+                for g in range(PASSES):
+                    first_product_pass(c, t, g)
+        round_w2(0)
+        negative_part(0)
+        positive_part(0)
+        round_w2(1)
+        quantize_w2(0)
+        negative_part(1)
+        positive_part(1)
+        join(0)
+        negative_part(2)
+        positive_part(2)
+        quantize_z(0)
+        quantize_w2(1)
+        join(1)
+        negative_part(3)
+        positive_part(3)
+        second_product(0, [0, 1, 2, 3], nc.scalar.copy, nc.sync)
+        quantize_z(1)
+        join(2)
+        second_product(1, [0, 1, 2, 3], nc.scalar.copy, nc.sync)
+        join(3)
+        quantize_z(2)
+        quantize_z(3)
+        second_product(2, [0, 1, 2, 3], nc.scalar.copy, nc.sync)
+        second_product(3, [0, 1], nc.vector.tensor_copy, nc.sync)
+        second_product(3, [2, 3], nc.vector.tensor_copy, nc.sync)

@@ -76,8 +76,14 @@ def tile_picked_prelu8_none_p_kernel(tc, x_words, x_scales, w1, slope, w2, offs,
         w1_bf = [sb(f"w1_bf{g}", [P, H * PACK], BF16) for g in range(PASSES)]
         for g in range(PASSES):
             nc.scalar.copy(
-                w1_bf[g][:].rearrange("p (t m j) -> p m j t", t=PACK, j=PACK),
-                w1_raw[g][:].rearrange("p j (m t) -> p m j t", t=PACK),
+                w1_bf[g][:].rearrange("p (a b m j) -> p a m j b", a=2, b=2, j=PACK),
+                w1_raw[g][:].rearrange("p j (m a b) -> p a m j b", a=2, b=2),
+            )
+        woven_slope = w1_raw[PASSES - 1][:].rearrange("p j c -> p (j c)").rearrange("p (s t) -> p s t", t=PACK)
+        for h in range(2):
+            nc.scalar.copy(
+                woven_slope[:, h * HALF : (h + 1) * HALF, :].rearrange("p (c i) t -> p c t i", i=2),
+                picked_slope[h][:].rearrange("p t (c i) -> p c t i", i=2),
             )
         x_picked_scales = sb("x_picked_scales", [P, S], U8)
         x_first = sb("x_first", [P, S], U32)
@@ -108,7 +114,7 @@ def tile_picked_prelu8_none_p_kernel(tc, x_words, x_scales, w1, slope, w2, offs,
 
         y = [psum_y.tile([P, PACK, CHUNK], F32, name="y") for c in range(CHUNKS)]
         below = [sb(f"below{c}", [P, CHUNK, PACK], BF16) for c in range(CHUNKS)]
-        above = [sb(f"above{c}", [P, CHUNK, PACK], BF16) for c in range(CHUNKS)]
+        above = [w2_raw[1][:, c, :].bitcast(BF16).rearrange("p (s t) -> p s t", t=PACK) for c in range(CHUNKS)]
         z_bf = [sb(f"z_bf{c}", [P, CHUNK * PACK], BF16) for c in range(CHUNKS)]
         z_codes = [sb(f"z_codes{c}", [P, CHUNK], U32) for c in range(CHUNKS)]
         z_scales = [sb(f"z_scales{c}", [P, CHUNK], U8) for c in range(CHUNKS)]
@@ -129,24 +135,23 @@ def tile_picked_prelu8_none_p_kernel(tc, x_words, x_scales, w1, slope, w2, offs,
             )
 
         def negative_part(c):
-            in_half = slice(c % 2 * CHUNK, (c % 2 + 1) * CHUNK)
             nc.vector.scalar_tensor_tensor(
                 out=below[c][:],
                 in0=y[c][:].rearrange("p t s -> p s t"),
                 scalar=0.0,
-                in1=picked_slope[c // 2][:, :, in_half].rearrange("p t s -> p s t"),
+                in1=woven_slope[:, c * CHUNK : (c + 1) * CHUNK, :],
                 op0=ALU.min,
                 op1=ALU.mult,
             )
 
         def positive_part(c):
-            nc.scalar.activation(out=above[c][:], in_=y[c][:].rearrange("p t s -> p s t"), func=RELU)
+            nc.scalar.activation(out=above[c], in_=y[c][:].rearrange("p t s -> p s t"), func=RELU)
 
         def join(c):
             nc.vector.tensor_tensor(
                 z_bf[c][:],
                 below[c][:].rearrange("p s t -> p (s t)"),
-                above[c][:].rearrange("p s t -> p (s t)"),
+                above[c].rearrange("p s t -> p (s t)"),
                 ALU.add,
             )
 
@@ -177,20 +182,20 @@ def tile_picked_prelu8_none_p_kernel(tc, x_words, x_scales, w1, slope, w2, offs,
                 for g in range(PASSES):
                     first_product_pass(c, t, g)
         round_w2(0)
+        round_w2(1)
         negative_part(0)
         positive_part(0)
-        round_w2(1)
         quantize_w2(0)
         negative_part(1)
         positive_part(1)
+        quantize_w2(1)
         join(0)
         negative_part(2)
         positive_part(2)
         quantize_z(0)
-        quantize_w2(1)
         join(1)
-        negative_part(3)
         positive_part(3)
+        negative_part(3)
         second_product(0, [0, 1, 2, 3], nc.scalar.copy, nc.sync)
         quantize_z(1)
         join(2)
@@ -200,4 +205,4 @@ def tile_picked_prelu8_none_p_kernel(tc, x_words, x_scales, w1, slope, w2, offs,
         quantize_z(3)
         second_product(2, [0, 1, 2, 3], nc.scalar.copy, nc.sync)
         second_product(3, [0, 1], nc.vector.tensor_copy, nc.sync)
-        second_product(3, [2, 3], nc.vector.tensor_copy, nc.sync)
+        second_product(3, [2, 3], nc.scalar.copy, nc.sync)

@@ -147,6 +147,16 @@ def tile_picked_prelu8_none_p_kernel(tc, x_words, x_scales, w1, slope, w2, offs,
         def positive_part(c):
             nc.scalar.activation(out=above[c], in_=y[c][:].rearrange("p t s -> p s t"), func=RELU)
 
+        def add_positive_part(c):
+            nc.vector.scalar_tensor_tensor(
+                out=z_bf[c][:].rearrange("p (s t) -> p s t", t=PACK),
+                in0=y[c][:].rearrange("p t s -> p s t"),
+                scalar=0.0,
+                in1=below[c][:],
+                op0=ALU.max,
+                op1=ALU.add,
+            )
+
         def join(c):
             nc.vector.tensor_tensor(
                 z_bf[c][:],
@@ -176,6 +186,17 @@ def tile_picked_prelu8_none_p_kernel(tc, x_words, x_scales, w1, slope, w2, offs,
 
         for c in range(CHUNKS):
             first_product_pass(c, 0, 0)
+        for n in range(2):
+            warm = psum_o.tile([P, S], F32, name="acc")
+            nc.tensor.matmul_mx(
+                out=warm[:],
+                lhsT=w1_codes[0][:, 0:P].bitcast(FP8X4),
+                lhsT_scale=w1_scales[0][:, 0:P],
+                rhs=x_first[:].bitcast(FP8X4),
+                rhs_scale=x_picked_scales[:],
+                start=True,
+                stop=True,
+            )
         for c in range(CHUNKS):
             first_product_pass(c, 0, 1)
             for t in range(1, PACK):
@@ -184,25 +205,24 @@ def tile_picked_prelu8_none_p_kernel(tc, x_words, x_scales, w1, slope, w2, offs,
         round_w2(0)
         round_w2(1)
         negative_part(0)
-        positive_part(0)
         quantize_w2(0)
+        add_positive_part(0)
         negative_part(1)
         positive_part(1)
-        quantize_w2(1)
-        join(0)
-        negative_part(2)
-        positive_part(2)
         quantize_z(0)
-        join(1)
+        quantize_w2(1)
+        positive_part(2)
         positive_part(3)
-        negative_part(3)
+        negative_part(2)
+        join(1)
         second_product(0, [0, 1, 2, 3], nc.scalar.copy, nc.sync)
         quantize_z(1)
         join(2)
         second_product(1, [0, 1, 2, 3], nc.scalar.copy, nc.sync)
-        join(3)
+        negative_part(3)
         quantize_z(2)
-        quantize_z(3)
+        join(3)
         second_product(2, [0, 1, 2, 3], nc.scalar.copy, nc.sync)
+        quantize_z(3)
         second_product(3, [0, 1], nc.vector.tensor_copy, nc.sync)
-        second_product(3, [2, 3], nc.scalar.copy, nc.sync)
+        second_product(3, [2, 3], nc.scalar.copy, nc.scalar)

@@ -38,7 +38,9 @@ def tile_picked_prelu8_none_p_kernel(tc, x_words, x_scales, w1, slope, w2, offs,
         offs_list = sb("offs_list", [P, S // 16], U16)
         slope_rows = [sb(f"slope_rows{t}", [P, U], F32) for t in range(PACK)]
         w1_raw = [sb(f"w1_raw{g}", [P, PACK, H], F32) for g in range(PASSES)]
-        w2_raw = [sb(f"w2_raw{h}", [P, PACK, N // 2], F32) for h in range(2)]
+        w2_raw = [
+            sb(f"w2_raw{h}", [P, PACK * N // 2], F32)[:].rearrange("p (j c) -> p j c", j=PACK) for h in range(2)
+        ]
         x_table = [sb(f"x_table{g}", [P, T], I32) for g in range(PASSES)]
         x_scale_table = sb("x_scale_table", [P, T], U8)
 
@@ -49,23 +51,23 @@ def tile_picked_prelu8_none_p_kernel(tc, x_words, x_scales, w1, slope, w2, offs,
         for t in range(PACK):
             nc.sync.dma_start(slope_rows[t][:], slope_view[:, t, :])
         w1_view = w1.rearrange("(g p j) c -> g p j c", p=P, j=PACK)
-        for g in range(PASSES):
-            nc.sync.dma_start(w1_raw[g][:], w1_view[g])
+        nc.sync.dma_start(w1_raw[0][:], w1_view[0])
         nc.sync.dma_start(offs_list[:], offs)
         for q in range(4):
-            nc.scalar.dma_start(
+            nc.sync.dma_start(
                 x_scale_table[32 * q : 32 * q + 4 * PASSES, :].bitcast(I32),
                 x_scales[:, 4 * q : 4 * q + 4, :].bitcast(I32),
             )
+        nc.sync.dma_start(w1_raw[1][:], w1_view[1])
         for g in range(PASSES):
             nc.sync.dma_start(x_table[g][:], x_words[g].rearrange("p n t -> p (n t)").bitcast(I32))
         w2_view = w2.rearrange("(p j) c -> p j c", j=PACK)
         for h in range(2):
-            nc.sync.dma_start(w2_raw[h][:], w2_view[:, :, h * (N // 2) : (h + 1) * (N // 2)])
+            nc.sync.dma_start(w2_raw[h], w2_view[:, :, h * (N // 2) : (h + 1) * (N // 2)])
 
         picked_slope = [sb(f"picked_slope{h}", [P, PACK, HALF], F32) for h in range(2)]
-        for t in range(PACK):
-            for h in range(2):
+        for h in range(2):
+            for t in range(PACK):
                 nc.vector.tensor_copy(
                     picked_slope[h][:, t, :],
                     slope_rows[t][:].indirect(task_list[:, h * HALF // 16 : (h + 1) * HALF // 16]),
@@ -74,17 +76,24 @@ def tile_picked_prelu8_none_p_kernel(tc, x_words, x_scales, w1, slope, w2, offs,
         w1_codes = [sb(f"w1_codes{g}", [P, H], U32) for g in range(PASSES)]
         w1_scales = [sb(f"w1_scales{g}", [P, H], U8) for g in range(PASSES)]
         w1_bf = [sb(f"w1_bf{g}", [P, H * PACK], BF16) for g in range(PASSES)]
+        woven_slope = [
+            sb("woven_first", [P, HALF, PACK], F32)[:],
+            w1_raw[PASSES - 1][:, 0:2, :].rearrange("p j c -> p (j c)").rearrange("p (s t) -> p s t", t=PACK),
+        ]
+
+        def weave(h, copy):
+            copy(
+                woven_slope[h].rearrange("p (c i) t -> p c t i", i=2),
+                picked_slope[h][:].rearrange("p t (c i) -> p c t i", i=2),
+            )
+
+        weave(0, nc.vector.tensor_copy)
         for g in range(PASSES):
             nc.scalar.copy(
                 w1_bf[g][:].rearrange("p (a b m j) -> p a m j b", a=2, b=2, j=PACK),
                 w1_raw[g][:].rearrange("p j (m a b) -> p a m j b", a=2, b=2),
             )
-        woven_slope = w1_raw[PASSES - 1][:].rearrange("p j c -> p (j c)").rearrange("p (s t) -> p s t", t=PACK)
-        for h in range(2):
-            nc.scalar.copy(
-                woven_slope[:, h * HALF : (h + 1) * HALF, :].rearrange("p (c i) t -> p c t i", i=2),
-                picked_slope[h][:].rearrange("p t (c i) -> p c t i", i=2),
-            )
+        weave(1, nc.scalar.copy)
         x_picked_scales = sb("x_picked_scales", [P, S], U8)
         x_first = sb("x_first", [P, S], U32)
         x_second = [sb(f"x_second{h}", [P, HALF], U32) for h in range(2)]
@@ -102,10 +111,10 @@ def tile_picked_prelu8_none_p_kernel(tc, x_words, x_scales, w1, slope, w2, offs,
         w2_scales = sb("w2_scales", [P, N], U8)
         w2_bf = [sb(f"w2_bf{h}", [P, N // 2 * PACK], BF16) for h in range(2)]
 
-        def round_w2(h):
-            nc.scalar.copy(
-                w2_bf[h][:].rearrange("p (c i j) -> p c j i", i=4, j=PACK),
-                w2_raw[h][:].rearrange("p j (c i) -> p c j i", i=4),
+        def round_w2(h, lo, hi, copy):
+            copy(
+                w2_bf[h][:, lo * PACK : hi * PACK].rearrange("p (c i j) -> p c j i", i=4, j=PACK),
+                w2_raw[h][:, :, lo:hi].rearrange("p j (c i) -> p c j i", i=4),
             )
 
         def quantize_w2(h):
@@ -113,8 +122,12 @@ def tile_picked_prelu8_none_p_kernel(tc, x_words, x_scales, w1, slope, w2, offs,
             nc.vector.quantize_mx(out=w2_codes[:, cols].bitcast(FP8X4), scales=w2_scales[:, cols], in_=w2_bf[h][:])
 
         y = [psum_y.tile([P, PACK, CHUNK], F32, name="y") for c in range(CHUNKS)]
-        below = [sb(f"below{c}", [P, CHUNK, PACK], BF16) for c in range(CHUNKS)]
-        above = [w2_raw[1][:, c, :].bitcast(BF16).rearrange("p (s t) -> p s t", t=PACK) for c in range(CHUNKS)]
+        def as_tokens(ap):
+            return ap.rearrange("p (s t) -> p s t", t=PACK)
+
+        spent = [[as_tokens(w2_raw[h][:, j, :].bitcast(BF16)) for j in range(PACK)] for h in range(2)]
+        below = spent[0][1:] + [sb("below_last", [P, CHUNK, PACK], BF16)[:]]
+        above = spent[0][:1] + spent[1][1:]
         z_bf = [sb(f"z_bf{c}", [P, CHUNK * PACK], BF16) for c in range(CHUNKS)]
         z_codes = [sb(f"z_codes{c}", [P, CHUNK], U32) for c in range(CHUNKS)]
         z_scales = [sb(f"z_scales{c}", [P, CHUNK], U8) for c in range(CHUNKS)]
@@ -136,10 +149,10 @@ def tile_picked_prelu8_none_p_kernel(tc, x_words, x_scales, w1, slope, w2, offs,
 
         def negative_part(c):
             nc.vector.scalar_tensor_tensor(
-                out=below[c][:],
+                out=below[c],
                 in0=y[c][:].rearrange("p t s -> p s t"),
                 scalar=0.0,
-                in1=woven_slope[:, c * CHUNK : (c + 1) * CHUNK, :],
+                in1=woven_slope[c // 2][:, c % 2 * CHUNK : (c % 2 + 1) * CHUNK, :],
                 op0=ALU.min,
                 op1=ALU.mult,
             )
@@ -147,20 +160,10 @@ def tile_picked_prelu8_none_p_kernel(tc, x_words, x_scales, w1, slope, w2, offs,
         def positive_part(c):
             nc.scalar.activation(out=above[c], in_=y[c][:].rearrange("p t s -> p s t"), func=RELU)
 
-        def add_positive_part(c):
-            nc.vector.scalar_tensor_tensor(
-                out=z_bf[c][:].rearrange("p (s t) -> p s t", t=PACK),
-                in0=y[c][:].rearrange("p t s -> p s t"),
-                scalar=0.0,
-                in1=below[c][:],
-                op0=ALU.max,
-                op1=ALU.add,
-            )
-
         def join(c):
             nc.vector.tensor_tensor(
                 z_bf[c][:],
-                below[c][:].rearrange("p s t -> p (s t)"),
+                below[c].rearrange("p s t -> p (s t)"),
                 above[c].rearrange("p s t -> p (s t)"),
                 ALU.add,
             )
@@ -169,7 +172,10 @@ def tile_picked_prelu8_none_p_kernel(tc, x_words, x_scales, w1, slope, w2, offs,
             nc.vector.quantize_mx(out=z_codes[c][:].bitcast(FP8X4), scales=z_scales[c][:], in_=z_bf[c][:])
 
         def second_product(c, tiles, copy, queue):
-            acc = psum_o.tile([P, len(tiles), CHUNK], F32, name="acc")
+            if c != 2:
+                acc = psum_o.tile([P, len(tiles), CHUNK], F32, name="acc")
+            else:
+                acc = psum_y.tile([P, len(tiles), CHUNK], F32, name="y")
             for n, i in enumerate(tiles):
                 nc.tensor.matmul_mx(
                     out=acc[:, n, :],
@@ -184,45 +190,53 @@ def tile_picked_prelu8_none_p_kernel(tc, x_words, x_scales, w1, slope, w2, offs,
             copy(result[:], acc[:])
             queue.dma_start(out_view[:, tiles[0] : tiles[-1] + 1, c * CHUNK : (c + 1) * CHUNK], result[:])
 
-        for c in range(CHUNKS):
-            first_product_pass(c, 0, 0)
-        for n in range(2):
-            warm = psum_o.tile([P, S], F32, name="acc")
+        def warm_up(pool, tag):
+            warm = pool.tile([P, S], F32, name=tag)
             nc.tensor.matmul_mx(
                 out=warm[:],
-                lhsT=w1_codes[0][:, 0:P].bitcast(FP8X4),
-                lhsT_scale=w1_scales[0][:, 0:P],
-                rhs=x_first[:].bitcast(FP8X4),
-                rhs_scale=x_picked_scales[:],
+                lhsT=w1_codes[1][:, 0:P].bitcast(FP8X4),
+                lhsT_scale=w1_scales[1][:, 0:P],
+                rhs=w1_codes[1][:].bitcast(FP8X4),
+                rhs_scale=w1_scales[1][:],
                 start=True,
                 stop=True,
             )
+
+        warm_up(psum_o, "acc")
+        for c in range(CHUNKS):
+            first_product_pass(c, 0, 0)
         for c in range(CHUNKS):
             first_product_pass(c, 0, 1)
             for t in range(1, PACK):
                 for g in range(PASSES):
                     first_product_pass(c, t, g)
-        round_w2(0)
-        round_w2(1)
-        negative_part(0)
+        round_w2(0, 0, 160, nc.vector.tensor_copy)
+        round_w2(0, 160, 2 * P, nc.scalar.copy)
+        positive_part(0)
         quantize_w2(0)
-        add_positive_part(0)
         negative_part(1)
-        positive_part(1)
-        quantize_z(0)
-        quantize_w2(1)
-        positive_part(2)
-        positive_part(3)
+        round_w2(1, 0, 2 * P, nc.scalar.copy)
+        negative_part(0)
         negative_part(2)
-        join(1)
-        second_product(0, [0, 1, 2, 3], nc.scalar.copy, nc.sync)
-        quantize_z(1)
-        join(2)
-        second_product(1, [0, 1, 2, 3], nc.scalar.copy, nc.sync)
+        positive_part(1)
+        join(0)
         negative_part(3)
-        quantize_z(2)
+        positive_part(2)
+        quantize_z(0)
+        warm_up(psum_y, "y")
+        warm_up(psum_y, "y")
+        second_product(0, [0, 1], nc.scalar.copy, nc.sync)
+        quantize_w2(1)
+        positive_part(3)
+        join(1)
+        second_product(0, [2, 3], nc.scalar.copy, nc.sync)
+        join(2)
+        quantize_z(1)
+        second_product(1, [0, 1, 2, 3], nc.scalar.copy, nc.sync)
         join(3)
-        second_product(2, [0, 1, 2, 3], nc.scalar.copy, nc.sync)
+        quantize_z(2)
         quantize_z(3)
+        second_product(2, [0, 1], nc.vector.tensor_copy, nc.sync)
+        second_product(2, [2, 3], nc.scalar.copy, nc.scalar)
         second_product(3, [0, 1], nc.vector.tensor_copy, nc.sync)
         second_product(3, [2, 3], nc.scalar.copy, nc.scalar)

@@ -44,7 +44,7 @@ def tile_picked_prelu8_none_p_kernel(tc, x_words, x_scales, w1, slope, w2, offs,
         x_table = [sb(f"x_table{g}", [P, T], I32) for g in range(PASSES)]
         x_scale_table = sb("x_scale_table", [P, T], U8)
 
-        nc.vector.memset(x_scale_table[:].bitcast(I32), 0)
+        nc.gpsimd.memset(x_scale_table[:].bitcast(I32), 0)
 
         nc.sync.dma_start(task_list[:], task)
         slope_view = slope.rearrange("(p t) u -> p t u", t=PACK)
@@ -54,7 +54,7 @@ def tile_picked_prelu8_none_p_kernel(tc, x_words, x_scales, w1, slope, w2, offs,
         nc.sync.dma_start(w1_raw[0][:], w1_view[0])
         nc.sync.dma_start(offs_list[:], offs)
         for q in range(4):
-            nc.sync.dma_start(
+            nc.gpsimd.dma_start(
                 x_scale_table[32 * q : 32 * q + 4 * PASSES, :].bitcast(I32),
                 x_scales[:, 4 * q : 4 * q + 4, :].bitcast(I32),
             )
@@ -77,7 +77,7 @@ def tile_picked_prelu8_none_p_kernel(tc, x_words, x_scales, w1, slope, w2, offs,
         w1_scales = [sb(f"w1_scales{g}", [P, H], U8) for g in range(PASSES)]
         w1_bf = [sb(f"w1_bf{g}", [P, H * PACK], BF16) for g in range(PASSES)]
         woven_slope = [
-            sb("woven_first", [P, HALF, PACK], F32)[:],
+            w1_raw[PASSES - 1][:, 2:4, :].rearrange("p j c -> p (j c)").rearrange("p (s t) -> p s t", t=PACK),
             w1_raw[PASSES - 1][:, 0:2, :].rearrange("p j c -> p (j c)").rearrange("p (s t) -> p s t", t=PACK),
         ]
 
@@ -87,12 +87,12 @@ def tile_picked_prelu8_none_p_kernel(tc, x_words, x_scales, w1, slope, w2, offs,
                 picked_slope[h][:].rearrange("p t (c i) -> p c t i", i=2),
             )
 
-        weave(0, nc.vector.tensor_copy)
         for g in range(PASSES):
             nc.scalar.copy(
                 w1_bf[g][:].rearrange("p (a b m j) -> p a m j b", a=2, b=2, j=PACK),
                 w1_raw[g][:].rearrange("p j (m a b) -> p a m j b", a=2, b=2),
             )
+        weave(0, nc.scalar.copy)
         weave(1, nc.scalar.copy)
         x_picked_scales = sb("x_picked_scales", [P, S], U8)
         x_first = sb("x_first", [P, S], U32)

@@ -46,9 +46,10 @@ def tile_picked_prelu8_none_p_kernel(tc, x_words, x_scales, w1, slope, w2, offs,
 
         nc.gpsimd.memset(x_scale_table[:].bitcast(I32), 0)
 
-        nc.sync.dma_start(task_list[:], task)
         slope_view = slope.rearrange("(p t) u -> p t u", t=PACK)
-        for t in range(PACK):
+        nc.sync.dma_start(slope_rows[0][:], slope_view[:, 0, :])
+        nc.sync.dma_start(task_list[:], task)
+        for t in range(1, PACK):
             nc.sync.dma_start(slope_rows[t][:], slope_view[:, t, :])
         w1_view = w1.rearrange("(g p j) c -> g p j c", p=P, j=PACK)
         nc.sync.dma_start(w1_raw[0][:], w1_view[0])
@@ -73,7 +74,7 @@ def tile_picked_prelu8_none_p_kernel(tc, x_words, x_scales, w1, slope, w2, offs,
                     slope_rows[t][:].indirect(task_list[:, h * HALF // 16 : (h + 1) * HALF // 16]),
                 )
 
-        w1_codes = [sb(f"w1_codes{g}", [P, H], U32) for g in range(PASSES)]
+        w1_codes = [sb(name, [P, H], U32) for name in ("w1_codes0", "x_table0")]
         w1_scales = [sb(f"w1_scales{g}", [P, H], U8) for g in range(PASSES)]
         w1_bf = [sb(f"w1_bf{g}", [P, H * PACK], BF16) for g in range(PASSES)]
         woven_slope = [
@@ -94,7 +95,7 @@ def tile_picked_prelu8_none_p_kernel(tc, x_words, x_scales, w1, slope, w2, offs,
             )
         weave(0, nc.scalar.copy)
         weave(1, nc.scalar.copy)
-        x_picked_scales = sb("x_picked_scales", [P, S], U8)
+        x_picked_scales = sb("w1_bf0", [P, S], U8)
         x_first = sb("x_first", [P, S], U32)
         x_second = [sb(f"x_second{h}", [P, HALF], U32) for h in range(2)]
         nc.vector.quantize_mx(out=w1_codes[0][:].bitcast(FP8X4), scales=w1_scales[0][:], in_=w1_bf[0][:])
@@ -122,82 +123,92 @@ def tile_picked_prelu8_none_p_kernel(tc, x_words, x_scales, w1, slope, w2, offs,
             nc.vector.quantize_mx(out=w2_codes[:, cols].bitcast(FP8X4), scales=w2_scales[:, cols], in_=w2_bf[h][:])
 
         y = [psum_y.tile([P, PACK, CHUNK], F32, name="y") for c in range(CHUNKS)]
-        def as_tokens(ap):
-            return ap.rearrange("p (s t) -> p s t", t=PACK)
 
-        spent = [[as_tokens(w2_raw[h][:, j, :].bitcast(BF16)) for j in range(PACK)] for h in range(2)]
-        below = spent[0][1:] + [sb("below_last", [P, CHUNK, PACK], BF16)[:]]
+        def in_two_runs(ap):
+            return ap.rearrange("p (a r) -> p a r", a=2)
+
+        spent = [[w2_raw[h][:, j, :].bitcast(BF16) for j in range(PACK)] for h in range(2)]
+        below = [in_two_runs(ap) for ap in spent[0][1:] + [sb("below_last", [P, CHUNK * PACK], BF16)[:]]]
         above = spent[0][:1] + spent[1][1:]
         z_bf = [sb(f"z_bf{c}", [P, CHUNK * PACK], BF16) for c in range(CHUNKS)]
-        z_codes = [sb(f"z_codes{c}", [P, CHUNK], U32) for c in range(CHUNKS)]
-        z_scales = [sb(f"z_scales{c}", [P, CHUNK], U8) for c in range(CHUNKS)]
+        z_codes = sb("z_codes", [P, S], U32)
+        z_scales = sb("z_scales", [P, S], U8)
         out_view = out.rearrange("(i p) s -> p i s", p=P)
 
+        def tokens(c, count=1):
+            return slice(c * CHUNK, (c + count) * CHUNK)
+
         def first_product_pass(c, t, g):
-            cols = slice(c * CHUNK, (c + 1) * CHUNK)
-            in_half = slice(c % 2 * CHUNK, (c % 2 + 1) * CHUNK)
-            moving = [x_first[:, cols], x_second[c // 2][:, in_half]]
+            moving = [x_first[:, tokens(c)], x_second[c // 2][:, tokens(c % 2)]]
             nc.tensor.matmul_mx(
                 out=y[c][:, t, :],
                 lhsT=w1_codes[g][:, t * P : (t + 1) * P].bitcast(FP8X4),
                 lhsT_scale=w1_scales[g][:, t * P : (t + 1) * P],
                 rhs=moving[g].bitcast(FP8X4),
-                rhs_scale=x_picked_scales[4 * g : P, cols],
+                rhs_scale=x_picked_scales[4 * g : P, tokens(c)],
                 start=(g == 0),
                 stop=(g == PASSES - 1),
             )
 
         def negative_part(c):
             nc.vector.scalar_tensor_tensor(
-                out=below[c],
-                in0=y[c][:].rearrange("p t s -> p s t"),
+                out=below[c].rearrange("p a (s t) -> p a s t", t=PACK),
+                in0=y[c][:].rearrange("p t (a s) -> p a s t", a=2),
                 scalar=0.0,
-                in1=woven_slope[c // 2][:, c % 2 * CHUNK : (c % 2 + 1) * CHUNK, :],
+                in1=woven_slope[c // 2][:, tokens(c % 2), :].rearrange("p (a s) t -> p a s t", a=2),
                 op0=ALU.min,
                 op1=ALU.mult,
             )
 
         def positive_part(c):
-            nc.scalar.activation(out=above[c], in_=y[c][:].rearrange("p t s -> p s t"), func=RELU)
-
-        def join(c):
-            nc.vector.tensor_tensor(
-                z_bf[c][:],
-                below[c].rearrange("p s t -> p (s t)"),
-                above[c].rearrange("p s t -> p (s t)"),
-                ALU.add,
+            nc.scalar.activation(
+                out=above[c].rearrange("p (s t) -> p s t", t=PACK),
+                in_=y[c][:].rearrange("p t s -> p s t"),
+                func=RELU,
             )
 
-        def quantize_z(c):
-            nc.vector.quantize_mx(out=z_codes[c][:].bitcast(FP8X4), scales=z_scales[c][:], in_=z_bf[c][:])
+        def add_positive_part(c):
+            nc.vector.scalar_tensor_tensor(
+                out=z_bf[c][:].rearrange("p (a s t) -> p a s t", a=2, t=PACK),
+                in0=y[c][:].rearrange("p t (a s) -> p a s t", a=2),
+                scalar=0.0,
+                in1=below[c].rearrange("p a (s t) -> p a s t", t=PACK),
+                op0=ALU.max,
+                op1=ALU.add,
+            )
 
-        def second_product(c, tiles, copy, queue):
-            if c != 2:
-                acc = psum_o.tile([P, len(tiles), CHUNK], F32, name="acc")
-            else:
-                acc = psum_y.tile([P, len(tiles), CHUNK], F32, name="y")
+        def join(c):
+            nc.vector.tensor_tensor(in_two_runs(z_bf[c][:]), below[c], in_two_runs(above[c]), ALU.add)
+
+        def quantize_z(c):
+            nc.vector.quantize_mx(
+                out=z_codes[:, tokens(c)].bitcast(FP8X4), scales=z_scales[:, tokens(c)], in_=z_bf[c][:]
+            )
+
+        def second_product(c, count, tiles, pool, tag, copy, queue):
+            acc = pool.tile([P, len(tiles), count * CHUNK], F32, name=tag)
             for n, i in enumerate(tiles):
                 nc.tensor.matmul_mx(
                     out=acc[:, n, :],
                     lhsT=w2_codes[:, i * P : (i + 1) * P].bitcast(FP8X4),
                     lhsT_scale=w2_scales[:, i * P : (i + 1) * P],
-                    rhs=z_codes[c][:].bitcast(FP8X4),
-                    rhs_scale=z_scales[c][:],
+                    rhs=z_codes[:, tokens(c, count)].bitcast(FP8X4),
+                    rhs_scale=z_scales[:, tokens(c, count)],
                     start=True,
                     stop=True,
                 )
-            result = sb(f"result{c}_{tiles[0]}", [P, len(tiles), CHUNK], F32)
+            result = sb(f"result{c}_{tiles[0]}", [P, len(tiles), count * CHUNK], F32)
             copy(result[:], acc[:])
-            queue.dma_start(out_view[:, tiles[0] : tiles[-1] + 1, c * CHUNK : (c + 1) * CHUNK], result[:])
+            queue.dma_start(out_view[:, tiles[0] : tiles[-1] + 1, tokens(c, count)], result[:])
 
         def warm_up(pool, tag):
             warm = pool.tile([P, S], F32, name=tag)
             nc.tensor.matmul_mx(
                 out=warm[:],
-                lhsT=w1_codes[1][:, 0:P].bitcast(FP8X4),
-                lhsT_scale=w1_scales[1][:, 0:P],
-                rhs=w1_codes[1][:].bitcast(FP8X4),
-                rhs_scale=w1_scales[1][:],
+                lhsT=w1_codes[0][:, 0:P].bitcast(FP8X4),
+                lhsT_scale=w1_scales[0][:, 0:P],
+                rhs=x_first[:].bitcast(FP8X4),
+                rhs_scale=x_picked_scales[:],
                 start=True,
                 stop=True,
             )
@@ -225,18 +236,19 @@ def tile_picked_prelu8_none_p_kernel(tc, x_words, x_scales, w1, slope, w2, offs,
         quantize_z(0)
         warm_up(psum_y, "y")
         warm_up(psum_y, "y")
-        second_product(0, [0, 1], nc.scalar.copy, nc.sync)
+        second_product(0, 1, [0, 1], psum_o, "acc", nc.scalar.copy, nc.sync)
         quantize_w2(1)
         positive_part(3)
         join(1)
-        second_product(0, [2, 3], nc.scalar.copy, nc.sync)
+        second_product(0, 1, [2, 3], psum_o, "acc", nc.scalar.copy, nc.sync)
         join(2)
         quantize_z(1)
-        second_product(1, [0, 1, 2, 3], nc.scalar.copy, nc.sync)
+        second_product(1, 1, [0, 1], psum_o, "acc", nc.scalar.copy, nc.sync)
         join(3)
         quantize_z(2)
         quantize_z(3)
-        second_product(2, [0, 1], nc.vector.tensor_copy, nc.sync)
-        second_product(2, [2, 3], nc.scalar.copy, nc.scalar)
-        second_product(3, [0, 1], nc.vector.tensor_copy, nc.sync)
-        second_product(3, [2, 3], nc.scalar.copy, nc.scalar)
+        second_product(1, 1, [2, 3], psum_o, "acc", nc.vector.tensor_copy, nc.sync)
+        second_product(2, 2, [0], psum_y, "y", nc.scalar.copy, nc.sync)
+        second_product(2, 2, [1], psum_y, "y", nc.vector.tensor_copy, nc.sync)
+        second_product(2, 2, [2], psum_o, "acc", nc.scalar.copy, nc.scalar)
+        second_product(2, 2, [3], psum_o, "acc", nc.vector.tensor_copy, nc.sync)

@@ -22,6 +22,7 @@ HALF = S // 2
 CHUNK = 128
 CHUNKS = S // CHUNK
 M_TILES = N // P
+EARLY = 2
 
 
 def tile_picked_prelu8_none_p_kernel(tc, x_words, x_scales, w1, slope, w2, offs, task, out):
@@ -146,8 +147,8 @@ def tile_picked_prelu8_none_p_kernel(tc, x_words, x_scales, w1, slope, w2, offs,
                 lhsT_scale=w1_scales[g][:, t * P : (t + 1) * P],
                 rhs=moving[g].bitcast(FP8X4),
                 rhs_scale=x_picked_scales[4 * g : P, tokens(c)],
-                start=(g == 0),
-                stop=(g == PASSES - 1),
+                start=(g == 0 and (t == 0 or c >= EARLY)),
+                stop=(g == PASSES - 1 and (t == PACK - 1 or c >= EARLY)),
             )
 
         def negative_part(c):
@@ -213,13 +214,13 @@ def tile_picked_prelu8_none_p_kernel(tc, x_words, x_scales, w1, slope, w2, offs,
                 stop=True,
             )
 
-        warm_up(psum_o, "acc")
         for c in range(CHUNKS):
-            first_product_pass(c, 0, 0)
+            for t in range(PACK if c < EARLY else 1):
+                first_product_pass(c, t, 0)
         for c in range(CHUNKS):
             first_product_pass(c, 0, 1)
             for t in range(1, PACK):
-                for g in range(PASSES):
+                for g in range(1 if c < EARLY else 0, PASSES):
                     first_product_pass(c, t, g)
         round_w2(0, 0, 160, nc.vector.tensor_copy)
         round_w2(0, 160, 2 * P, nc.scalar.copy)
@@ -234,6 +235,7 @@ def tile_picked_prelu8_none_p_kernel(tc, x_words, x_scales, w1, slope, w2, offs,
         negative_part(3)
         positive_part(2)
         quantize_z(0)
+        warm_up(psum_y, "y")
         warm_up(psum_y, "y")
         warm_up(psum_y, "y")
         second_product(0, 1, [0, 1], psum_o, "acc", nc.scalar.copy, nc.sync)

@@ -79,7 +79,7 @@ def tile_picked_prelu8_none_p_kernel(tc, x_words, x_scales, w1, slope, w2, offs,
         w1_scales = [sb(f"w1_scales{g}", [P, H], U8) for g in range(PASSES)]
         w1_bf = [sb(f"w1_bf{g}", [P, H * PACK], BF16) for g in range(PASSES)]
         woven_slope = [
-            w1_raw[PASSES - 1][:, 2:4, :].rearrange("p j c -> p (j c)").rearrange("p (s t) -> p s t", t=PACK),
+            sb("woven_first", [P, HALF, PACK], F32)[:],
             w1_raw[PASSES - 1][:, 0:2, :].rearrange("p j c -> p (j c)").rearrange("p (s t) -> p s t", t=PACK),
         ]
 
@@ -94,7 +94,7 @@ def tile_picked_prelu8_none_p_kernel(tc, x_words, x_scales, w1, slope, w2, offs,
                 w1_bf[g][:].rearrange("p (a b m j) -> p a m j b", a=2, b=2, j=PACK),
                 w1_raw[g][:].rearrange("p j (m a b) -> p a m j b", a=2, b=2),
             )
-        weave(0, nc.scalar.copy)
+        weave(0, nc.vector.tensor_copy)
         weave(1, nc.scalar.copy)
         x_picked_scales = sb("w1_bf0", [P, S], U8)
         x_first = sb("x_first", [P, S], U32)

@@ -22,14 +22,14 @@ HALF = S // 2
 CHUNK = 128
 CHUNKS = S // CHUNK
 M_TILES = N // P
-EARLY = 2
+EARLY = 3
 
 
 def tile_picked_prelu8_none_p_kernel(tc, x_words, x_scales, w1, slope, w2, offs, task, out):
     nc = tc.nc
     with ExitStack() as ctx:
         keep = ctx.enter_context(tc.tile_pool(name="keep", bufs=1))
-        psum_y = ctx.enter_context(tc.psum_pool(name="psum_y", bufs=4))
+        psum_y = ctx.enter_context(tc.psum_pool(name="psum_y", bufs=1))
         psum_o = ctx.enter_context(tc.psum_pool(name="psum_o", bufs=4))
 
         def sb(name, shape, dtype):
@@ -45,7 +45,7 @@ def tile_picked_prelu8_none_p_kernel(tc, x_words, x_scales, w1, slope, w2, offs,
         x_table = [sb(f"x_table{g}", [P, T], I32) for g in range(PASSES)]
         x_scale_table = sb("x_scale_table", [P, T], U8)
 
-        nc.gpsimd.memset(x_scale_table[:].bitcast(I32), 0)
+        nc.vector.memset(x_scale_table[:].bitcast(I32), 0)
 
         slope_view = slope.rearrange("(p t) u -> p t u", t=PACK)
         nc.sync.dma_start(slope_rows[0][:], slope_view[:, 0, :])
@@ -97,16 +97,21 @@ def tile_picked_prelu8_none_p_kernel(tc, x_words, x_scales, w1, slope, w2, offs,
         weave(0, nc.vector.tensor_copy)
         weave(1, nc.scalar.copy)
         x_picked_scales = sb("w1_bf0", [P, S], U8)
-        x_first = sb("x_first", [P, S], U32)
-        x_second = [sb(f"x_second{h}", [P, HALF], U32) for h in range(2)]
+        x_first = [sb(f"x_first{h}", [P, HALF], U32) for h in range(2)]
+        pieces = [(0, 1), (1, 1), (2, 2)]
+        x_second = [sb(f"x_second{c}", [P, count * CHUNK], U32) for c, count in pieces]
         nc.vector.quantize_mx(out=w1_codes[0][:].bitcast(FP8X4), scales=w1_scales[0][:], in_=w1_bf[0][:])
         nc.vector.tensor_copy(x_picked_scales[:], x_scale_table[:].indirect(offs_list[:]))
-        nc.vector.tensor_copy(x_first[:], x_table[0][:].bitcast(U32).indirect(offs_list[:]))
-        nc.vector.quantize_mx(out=w1_codes[1][:].bitcast(FP8X4), scales=w1_scales[1][:], in_=w1_bf[1][:])
         for h in range(2):
             nc.vector.tensor_copy(
-                x_second[h][:],
-                x_table[1][:].bitcast(U32).indirect(offs_list[:, h * HALF // 16 : (h + 1) * HALF // 16]),
+                x_first[h][:],
+                x_table[0][:].bitcast(U32).indirect(offs_list[:, h * HALF // 16 : (h + 1) * HALF // 16]),
+            )
+        nc.vector.quantize_mx(out=w1_codes[1][:].bitcast(FP8X4), scales=w1_scales[1][:], in_=w1_bf[1][:])
+        for picked, (c, count) in zip(x_second, pieces):
+            nc.vector.tensor_copy(
+                picked[:],
+                x_table[1][:].bitcast(U32).indirect(offs_list[:, c * CHUNK // 16 : (c + count) * CHUNK // 16]),
             )
 
         w2_codes = sb("w2_codes", [P, N], U32)
@@ -119,19 +124,25 @@ def tile_picked_prelu8_none_p_kernel(tc, x_words, x_scales, w1, slope, w2, offs,
                 w2_raw[h][:, :, lo:hi].rearrange("p j (c i) -> p c j i", i=4),
             )
 
+        def round_w2_on_gpsimd(h):
+            nc.gpsimd.tensor_scalar(
+                w2_bf[h][:].rearrange("p (c j) -> p c j", j=PACK),
+                w2_raw[h].rearrange("p j c -> p c j"),
+                1.0,
+                0.0,
+                ALU.mult,
+                ALU.add,
+            )
+
         def quantize_w2(h):
             cols = slice(h * (N // 2), (h + 1) * (N // 2))
             nc.vector.quantize_mx(out=w2_codes[:, cols].bitcast(FP8X4), scales=w2_scales[:, cols], in_=w2_bf[h][:])
 
-        y = [psum_y.tile([P, PACK, CHUNK], F32, name="y") for c in range(CHUNKS)]
-
-        def in_two_runs(ap):
-            return ap.rearrange("p (a r) -> p a r", a=2)
-
-        spent = [[w2_raw[h][:, j, :].bitcast(BF16) for j in range(PACK)] for h in range(2)]
-        below = [in_two_runs(ap) for ap in spent[0][1:] + [sb("below_last", [P, CHUNK * PACK], BF16)[:]]]
-        above = spent[0][:1] + spent[1][1:]
-        z_bf = [sb(f"z_bf{c}", [P, CHUNK * PACK], BF16) for c in range(CHUNKS)]
+        y = [psum_y.tile([P, PACK, CHUNK], F32, name=f"y{c}") for c in range(CHUNKS - 1)]
+        below = [sb(f"below{c}", [P, CHUNK * PACK], BF16)[:] for c in range(CHUNKS - 1)]
+        above = [sb(f"above{c}", [P, CHUNK * PACK], BF16)[:] for c in range(2)]
+        above = above + [w2_raw[1][:, j, :].bitcast(BF16) for j in range(2)]
+        z_bf = [sb(f"z_bf{c}", [P, CHUNK * PACK], BF16)[:] for c in range(CHUNKS)]
         z_codes = sb("z_codes", [P, S], U32)
         z_scales = sb("z_scales", [P, S], U8)
         out_view = out.rearrange("(i p) s -> p i s", p=P)
@@ -140,7 +151,7 @@ def tile_picked_prelu8_none_p_kernel(tc, x_words, x_scales, w1, slope, w2, offs,
             return slice(c * CHUNK, (c + count) * CHUNK)
 
         def first_product_pass(c, t, g):
-            moving = [x_first[:, tokens(c)], x_second[c // 2][:, tokens(c % 2)]]
+            moving = [x_first[c // 2][:, tokens(c % 2)], x_second[min(c, 2)][:, tokens(max(c - 2, 0))]]
             nc.tensor.matmul_mx(
                 out=y[c][:, t, :],
                 lhsT=w1_codes[g][:, t * P : (t + 1) * P].bitcast(FP8X4),
@@ -153,10 +164,10 @@ def tile_picked_prelu8_none_p_kernel(tc, x_words, x_scales, w1, slope, w2, offs,
 
         def negative_part(c):
             nc.vector.scalar_tensor_tensor(
-                out=below[c].rearrange("p a (s t) -> p a s t", t=PACK),
-                in0=y[c][:].rearrange("p t (a s) -> p a s t", a=2),
+                out=below[c].rearrange("p (s t) -> p s t", t=PACK),
+                in0=y[c][:].rearrange("p t s -> p s t"),
                 scalar=0.0,
-                in1=woven_slope[c // 2][:, tokens(c % 2), :].rearrange("p (a s) t -> p a s t", a=2),
+                in1=woven_slope[c // 2][:, tokens(c % 2), :],
                 op0=ALU.min,
                 op1=ALU.mult,
             )
@@ -168,23 +179,11 @@ def tile_picked_prelu8_none_p_kernel(tc, x_words, x_scales, w1, slope, w2, offs,
                 func=RELU,
             )
 
-        def add_positive_part(c):
-            nc.vector.scalar_tensor_tensor(
-                out=z_bf[c][:].rearrange("p (a s t) -> p a s t", a=2, t=PACK),
-                in0=y[c][:].rearrange("p t (a s) -> p a s t", a=2),
-                scalar=0.0,
-                in1=below[c].rearrange("p a (s t) -> p a s t", t=PACK),
-                op0=ALU.max,
-                op1=ALU.add,
-            )
-
         def join(c):
-            nc.vector.tensor_tensor(in_two_runs(z_bf[c][:]), below[c], in_two_runs(above[c]), ALU.add)
+            nc.vector.tensor_tensor(z_bf[c], below[c], above[c], ALU.add)
 
         def quantize_z(c):
-            nc.vector.quantize_mx(
-                out=z_codes[:, tokens(c)].bitcast(FP8X4), scales=z_scales[:, tokens(c)], in_=z_bf[c][:]
-            )
+            nc.vector.quantize_mx(out=z_codes[:, tokens(c)].bitcast(FP8X4), scales=z_scales[:, tokens(c)], in_=z_bf[c])
 
         def second_product(c, count, tiles, pool, tag, copy, queue):
             acc = pool.tile([P, len(tiles), count * CHUNK], F32, name=tag)
@@ -202,55 +201,38 @@ def tile_picked_prelu8_none_p_kernel(tc, x_words, x_scales, w1, slope, w2, offs,
             copy(result[:], acc[:])
             queue.dma_start(out_view[:, tiles[0] : tiles[-1] + 1, tokens(c, count)], result[:])
 
-        def warm_up(pool, tag):
-            warm = pool.tile([P, S], F32, name=tag)
-            nc.tensor.matmul_mx(
-                out=warm[:],
-                lhsT=w1_codes[0][:, 0:P].bitcast(FP8X4),
-                lhsT_scale=w1_scales[0][:, 0:P],
-                rhs=x_first[:].bitcast(FP8X4),
-                rhs_scale=x_picked_scales[:],
-                start=True,
-                stop=True,
-            )
-
-        for c in range(CHUNKS):
-            for t in range(PACK if c < EARLY else 1):
-                first_product_pass(c, t, 0)
-        for c in range(CHUNKS):
-            first_product_pass(c, 0, 1)
-            for t in range(1, PACK):
-                for g in range(1 if c < EARLY else 0, PASSES):
+        for g in range(PASSES):
+            for c in range(EARLY):
+                for t in range(PACK):
                     first_product_pass(c, t, g)
-        round_w2(0, 0, 160, nc.vector.tensor_copy)
-        round_w2(0, 160, 2 * P, nc.scalar.copy)
+        round_w2_on_gpsimd(0)
+        negative_part(0)
+        positive_part(1)
+        negative_part(2)
         positive_part(0)
-        quantize_w2(0)
+        y.append(psum_y.tile([P, PACK, CHUNK], F32, name="y0"))
+        for t in range(PACK):
+            for g in range(PASSES):
+                first_product_pass(3, t, g)
         negative_part(1)
         round_w2(1, 0, 2 * P, nc.scalar.copy)
-        negative_part(0)
-        negative_part(2)
-        positive_part(1)
-        join(0)
-        negative_part(3)
-        positive_part(2)
-        quantize_z(0)
-        warm_up(psum_y, "y")
-        warm_up(psum_y, "y")
-        warm_up(psum_y, "y")
-        second_product(0, 1, [0, 1], psum_o, "acc", nc.scalar.copy, nc.sync)
-        quantize_w2(1)
         positive_part(3)
+        positive_part(2)
+        quantize_w2(0)
+        join(0)
         join(1)
-        second_product(0, 1, [2, 3], psum_o, "acc", nc.scalar.copy, nc.sync)
-        join(2)
+        quantize_z(0)
         quantize_z(1)
-        second_product(1, 1, [0, 1], psum_o, "acc", nc.scalar.copy, nc.sync)
+        second_product(0, 2, [0, 1], psum_o, "acc", nc.scalar.copy, nc.sync)
+        quantize_w2(1)
+        second_product(0, 2, [2, 3], psum_o, "acc", nc.scalar.copy, nc.sync)
+        below.append(sb("z_bf0", [P, CHUNK * PACK], BF16)[:])
+        negative_part(3)
+        join(2)
         join(3)
         quantize_z(2)
         quantize_z(3)
-        second_product(1, 1, [2, 3], psum_o, "acc", nc.vector.tensor_copy, nc.sync)
-        second_product(2, 2, [0], psum_y, "y", nc.scalar.copy, nc.sync)
-        second_product(2, 2, [1], psum_y, "y", nc.vector.tensor_copy, nc.sync)
-        second_product(2, 2, [2], psum_o, "acc", nc.scalar.copy, nc.scalar)
-        second_product(2, 2, [3], psum_o, "acc", nc.vector.tensor_copy, nc.sync)
+        second_product(2, 2, [0], psum_o, "acc", nc.vector.tensor_copy, nc.sync)
+        second_product(2, 2, [1], psum_o, "acc", nc.scalar.copy, nc.scalar)
+        second_product(2, 2, [2], psum_y, "y1", nc.vector.tensor_copy, nc.sync)
+        second_product(2, 2, [3], psum_y, "y2", nc.scalar.copy, nc.scalar)

@@ -21,134 +21,110 @@ PASSES = K // (P * PACK)
 HALF = S // 2
 CHUNK = 128
 CHUNKS = S // CHUNK
-M_TILES = N // P
-EARLY = 3
+LAST = CHUNKS - 1
 
 
 def tile_picked_prelu8_none_p_kernel(tc, x_words, x_scales, w1, slope, w2, offs, task, out):
     nc = tc.nc
     with ExitStack() as ctx:
         keep = ctx.enter_context(tc.tile_pool(name="keep", bufs=1))
-        psum_y = ctx.enter_context(tc.psum_pool(name="psum_y", bufs=1))
-        psum_o = ctx.enter_context(tc.psum_pool(name="psum_o", bufs=4))
+        psum = ctx.enter_context(tc.psum_pool(name="psum", bufs=1))
 
         def sb(name, shape, dtype):
             return keep.tile(shape, dtype, name=name, align_bytes=64)
+
+        def entries(first, count):
+            return slice(first // 16, (first + count) // 16)
+
+        def tokens(c, count=1):
+            return slice(c * CHUNK, (c + count) * CHUNK)
 
         task_list = sb("task_list", [P, S // 16], U16)
         offs_list = sb("offs_list", [P, S // 16], U16)
         slope_rows = [sb(f"slope_rows{t}", [P, U], F32) for t in range(PACK)]
         w1_raw = [sb(f"w1_raw{g}", [P, PACK, H], F32) for g in range(PASSES)]
-        w2_raw = [
-            sb(f"w2_raw{h}", [P, PACK * N // 2], F32)[:].rearrange("p (j c) -> p j c", j=PACK) for h in range(2)
-        ]
+        w2_raw = [sb(f"w2_raw{h}", [P, PACK, N // 2], F32) for h in range(2)]
         x_table = [sb(f"x_table{g}", [P, T], I32) for g in range(PASSES)]
-        x_scale_table = sb("x_scale_table", [P, T], U8)
+        scale_table = sb("scale_table", [P, T], U8)
 
-        nc.vector.memset(x_scale_table[:].bitcast(I32), 0)
+        nc.vector.memset(scale_table[:].bitcast(I32), 0)
 
         slope_view = slope.rearrange("(p t) u -> p t u", t=PACK)
+        w1_view = w1.rearrange("(g p j) c -> g p j c", p=P, j=PACK)
+        w2_view = w2.rearrange("(p j) c -> p j c", j=PACK)
         nc.sync.dma_start(slope_rows[0][:], slope_view[:, 0, :])
         nc.sync.dma_start(task_list[:], task)
-        for t in range(1, PACK):
-            nc.sync.dma_start(slope_rows[t][:], slope_view[:, t, :])
-        w1_view = w1.rearrange("(g p j) c -> g p j c", p=P, j=PACK)
-        nc.sync.dma_start(w1_raw[0][:], w1_view[0])
+        nc.sync.dma_start(slope_rows[1][:], slope_view[:, 1, :])
         nc.sync.dma_start(offs_list[:], offs)
-        for q in range(4):
-            nc.gpsimd.dma_start(
-                x_scale_table[32 * q : 32 * q + 4 * PASSES, :].bitcast(I32),
-                x_scales[:, 4 * q : 4 * q + 4, :].bitcast(I32),
-            )
-        nc.sync.dma_start(w1_raw[1][:], w1_view[1])
+        for g in range(PASSES):
+            nc.sync.dma_start(scale_table[4 * g : P : 8, :].bitcast(I32), x_scales[g].bitcast(I32))
+        for t in range(2, PACK):
+            nc.sync.dma_start(slope_rows[t][:], slope_view[:, t, :])
+        for g in range(PASSES):
+            nc.sync.dma_start(w1_raw[g][:], w1_view[g])
         for g in range(PASSES):
             nc.sync.dma_start(x_table[g][:], x_words[g].rearrange("p n t -> p (n t)").bitcast(I32))
-        w2_view = w2.rearrange("(p j) c -> p j c", j=PACK)
         for h in range(2):
-            nc.sync.dma_start(w2_raw[h], w2_view[:, :, h * (N // 2) : (h + 1) * (N // 2)])
+            nc.sync.dma_start(w2_raw[h][:], w2_view[:, :, h * (N // 2) : (h + 1) * (N // 2)])
 
         picked_slope = [sb(f"picked_slope{h}", [P, PACK, HALF], F32) for h in range(2)]
-        for h in range(2):
-            for t in range(PACK):
+
+        def pick_slopes(t):
+            for h in range(2):
                 nc.vector.tensor_copy(
-                    picked_slope[h][:, t, :],
-                    slope_rows[t][:].indirect(task_list[:, h * HALF // 16 : (h + 1) * HALF // 16]),
+                    picked_slope[h][:, t, :], slope_rows[t][:].indirect(task_list[:, entries(h * HALF, HALF)])
                 )
 
-        w1_codes = [sb(name, [P, H], U32) for name in ("w1_codes0", "x_table0")]
-        w1_scales = [sb(f"w1_scales{g}", [P, H], U8) for g in range(PASSES)]
-        w1_bf = [sb(f"w1_bf{g}", [P, H * PACK], BF16) for g in range(PASSES)]
-        woven_slope = [
-            sb("woven_first", [P, HALF, PACK], F32)[:],
-            w1_raw[PASSES - 1][:, 0:2, :].rearrange("p j c -> p (j c)").rearrange("p (s t) -> p s t", t=PACK),
-        ]
+        picked_scales = sb("picked_scales", [P, S], U8)
+        x_plane = sb("x_plane", [P, S], U8)
+        pick_slopes(0)
+        pick_slopes(1)
+        nc.vector.tensor_copy(picked_scales[:], scale_table[:].indirect(offs_list[:]))
+        pick_slopes(2)
+        nc.vector.tensor_copy(x_plane[:].bitcast(I32), picked_scales[:].bitcast(I32))
+        for g in range(PASSES):
+            for i in range(1, 4):
+                nc.gpsimd.dma_start(
+                    x_plane[4 * g + i : P : 32, :].bitcast(I32),
+                    picked_scales[4 * g + 8 * i : P : 32, :].bitcast(I32),
+                )
+        pick_slopes(3)
 
-        def weave(h, copy):
+        woven = [sb(f"woven{c}", [P, CHUNK, PACK], F32) for c in range(CHUNKS)]
+
+        def weave(c, copy):
             copy(
-                woven_slope[h].rearrange("p (c i) t -> p c t i", i=2),
-                picked_slope[h][:].rearrange("p t (c i) -> p c t i", i=2),
+                woven[c][:].rearrange("p (c i) t -> p c t i", i=2),
+                picked_slope[c // 2][:, :, tokens(c % 2)].rearrange("p t (c i) -> p c t i", i=2),
             )
 
+        w1_bf = [sb(f"w1_bf{g}", [P, H * PACK], BF16) for g in range(PASSES)]
         for g in range(PASSES):
             nc.scalar.copy(
                 w1_bf[g][:].rearrange("p (a b m j) -> p a m j b", a=2, b=2, j=PACK),
                 w1_raw[g][:].rearrange("p j (m a b) -> p a m j b", a=2, b=2),
             )
-        weave(0, nc.vector.tensor_copy)
-        weave(1, nc.scalar.copy)
-        x_picked_scales = sb("w1_bf0", [P, S], U8)
-        x_first = [sb(f"x_first{h}", [P, HALF], U32) for h in range(2)]
-        pieces = [(0, 1), (1, 1), (2, 2)]
-        x_second = [sb(f"x_second{c}", [P, count * CHUNK], U32) for c, count in pieces]
+        for c in range(CHUNKS):
+            weave(c, nc.vector.tensor_copy if c < 4 else nc.scalar.copy)
+
+        w1_scales = [sb(f"w1_scales{g}", [P, H], U8) for g in range(PASSES)]
+        w1_codes = [sb("w1_codes0", [P, H], U32)]
         nc.vector.quantize_mx(out=w1_codes[0][:].bitcast(FP8X4), scales=w1_scales[0][:], in_=w1_bf[0][:])
-        nc.vector.tensor_copy(x_picked_scales[:], x_scale_table[:].indirect(offs_list[:]))
+        x_first = [sb(f"x_first{h}", [P, HALF], U32) for h in range(2)]
         for h in range(2):
             nc.vector.tensor_copy(
-                x_first[h][:],
-                x_table[0][:].bitcast(U32).indirect(offs_list[:, h * HALF // 16 : (h + 1) * HALF // 16]),
+                x_first[h][:], x_table[0][:].bitcast(U32).indirect(offs_list[:, entries(h * HALF, HALF)])
             )
+        w1_codes.append(sb("x_table0", [P, H], U32))
         nc.vector.quantize_mx(out=w1_codes[1][:].bitcast(FP8X4), scales=w1_scales[1][:], in_=w1_bf[1][:])
+        pieces = [(0, 1), (1, 1), (2, 2)]
+        x_second = [sb(f"x_second{c}", [P, count * CHUNK], U32) for c, count in pieces]
         for picked, (c, count) in zip(x_second, pieces):
             nc.vector.tensor_copy(
-                picked[:],
-                x_table[1][:].bitcast(U32).indirect(offs_list[:, c * CHUNK // 16 : (c + count) * CHUNK // 16]),
+                picked[:], x_table[1][:].bitcast(U32).indirect(offs_list[:, entries(c * CHUNK, count * CHUNK)])
             )
 
-        w2_codes = sb("w2_codes", [P, N], U32)
-        w2_scales = sb("w2_scales", [P, N], U8)
-        w2_bf = [sb(f"w2_bf{h}", [P, N // 2 * PACK], BF16) for h in range(2)]
-
-        def round_w2(h, lo, hi, copy):
-            copy(
-                w2_bf[h][:, lo * PACK : hi * PACK].rearrange("p (c i j) -> p c j i", i=4, j=PACK),
-                w2_raw[h][:, :, lo:hi].rearrange("p j (c i) -> p c j i", i=4),
-            )
-
-        def round_w2_on_gpsimd(h):
-            nc.gpsimd.tensor_scalar(
-                w2_bf[h][:].rearrange("p (c j) -> p c j", j=PACK),
-                w2_raw[h].rearrange("p j c -> p c j"),
-                1.0,
-                0.0,
-                ALU.mult,
-                ALU.add,
-            )
-
-        def quantize_w2(h):
-            cols = slice(h * (N // 2), (h + 1) * (N // 2))
-            nc.vector.quantize_mx(out=w2_codes[:, cols].bitcast(FP8X4), scales=w2_scales[:, cols], in_=w2_bf[h][:])
-
-        y = [psum_y.tile([P, PACK, CHUNK], F32, name=f"y{c}") for c in range(CHUNKS - 1)]
-        below = [sb(f"below{c}", [P, CHUNK * PACK], BF16)[:] for c in range(CHUNKS - 1)]
-        above = [sb(f"above{c}", [P, CHUNK * PACK], BF16)[:] for c in range(2)]
-        above = above + [w2_raw[1][:, j, :].bitcast(BF16) for j in range(2)]
-        z_bf = [sb(f"z_bf{c}", [P, CHUNK * PACK], BF16)[:] for c in range(CHUNKS)]
-        z_codes = sb("z_codes", [P, S], U32)
-        z_scales = sb("z_scales", [P, S], U8)
-        out_view = out.rearrange("(i p) s -> p i s", p=P)
-
-        def tokens(c, count=1):
-            return slice(c * CHUNK, (c + count) * CHUNK)
+        y = [psum.tile([P, PACK, CHUNK], F32, name=f"bank{c}") for c in range(LAST)]
 
         def first_product_pass(c, t, g):
             moving = [x_first[c // 2][:, tokens(c % 2)], x_second[min(c, 2)][:, tokens(max(c - 2, 0))]]
@@ -157,82 +133,110 @@ def tile_picked_prelu8_none_p_kernel(tc, x_words, x_scales, w1, slope, w2, offs,
                 lhsT=w1_codes[g][:, t * P : (t + 1) * P].bitcast(FP8X4),
                 lhsT_scale=w1_scales[g][:, t * P : (t + 1) * P],
                 rhs=moving[g].bitcast(FP8X4),
-                rhs_scale=x_picked_scales[4 * g : P, tokens(c)],
-                start=(g == 0 and (t == 0 or c >= EARLY)),
-                stop=(g == PASSES - 1 and (t == PACK - 1 or c >= EARLY)),
+                rhs_scale=x_plane[4 * g : P, tokens(c)],
+                start=(g == 0 and t == 0),
+                stop=(g == PASSES - 1 and t == PACK - 1),
             )
+
+        for g in range(PASSES):
+            for c in range(LAST):
+                for t in range(PACK):
+                    first_product_pass(c, t, g)
+
+        def by_token(ap):
+            return ap.rearrange("p (s t) -> p s t", t=PACK)
+
+        def sums(c):
+            return y[c][:].rearrange("p t s -> p s t")
+
+        below = [sb(f"below{c}", [P, CHUNK * PACK], BF16) for c in range(LAST)]
+        above = [sb(f"above{c}", [P, CHUNK * PACK], BF16) for c in range(LAST)]
+        z_early = sb("z_early", [P, 2 * CHUNK * PACK], BF16)
+        z_bf = [z_early[:, : CHUNK * PACK], z_early[:, CHUNK * PACK :]]
+        z_bf = z_bf + [sb(f"z_late{c}", [P, CHUNK * PACK], BF16)[:] for c in (2, 3)]
+        z_codes = [sb(f"z_codes{h}", [P, HALF], U32) for h in range(2)]
+        z_scales = [sb(f"z_scales{h}", [P, HALF], U8) for h in range(2)]
+        w2_scales = [sb(f"w2_scales{h}", [P, N // 2], U8) for h in range(2)]
+        out_view = out.rearrange("(i p) s -> p i s", p=P)
 
         def negative_part(c):
             nc.vector.scalar_tensor_tensor(
-                out=below[c].rearrange("p (s t) -> p s t", t=PACK),
-                in0=y[c][:].rearrange("p t s -> p s t"),
-                scalar=0.0,
-                in1=woven_slope[c // 2][:, tokens(c % 2), :],
-                op0=ALU.min,
-                op1=ALU.mult,
+                out=by_token(below[c][:]), in0=sums(c), scalar=0.0, in1=woven[c][:], op0=ALU.min, op1=ALU.mult
             )
 
         def positive_part(c):
-            nc.scalar.activation(
-                out=above[c].rearrange("p (s t) -> p s t", t=PACK),
-                in_=y[c][:].rearrange("p t s -> p s t"),
-                func=RELU,
-            )
+            nc.scalar.activation(out=by_token(above[c][:]), in_=sums(c), func=RELU)
 
         def join(c):
-            nc.vector.tensor_tensor(z_bf[c], below[c], above[c], ALU.add)
+            nc.vector.tensor_tensor(z_bf[c], below[c][:], above[c][:], ALU.add)
 
-        def quantize_z(c):
-            nc.vector.quantize_mx(out=z_codes[:, tokens(c)].bitcast(FP8X4), scales=z_scales[:, tokens(c)], in_=z_bf[c])
+        def quantize_w2(h):
+            nc.vector.quantize_mx(out=w2_codes[h][:].bitcast(FP8X4), scales=w2_scales[h][:], in_=w2_bf[h][:])
 
-        def second_product(c, count, tiles, pool, tag, copy, queue):
-            acc = pool.tile([P, len(tiles), count * CHUNK], F32, name=tag)
+        def second_product(h, tiles, bank, copy, queue):
+            acc = psum.tile([P, len(tiles), HALF], F32, name=bank)
             for n, i in enumerate(tiles):
                 nc.tensor.matmul_mx(
                     out=acc[:, n, :],
-                    lhsT=w2_codes[:, i * P : (i + 1) * P].bitcast(FP8X4),
-                    lhsT_scale=w2_scales[:, i * P : (i + 1) * P],
-                    rhs=z_codes[:, tokens(c, count)].bitcast(FP8X4),
-                    rhs_scale=z_scales[:, tokens(c, count)],
+                    lhsT=w2_codes[i // 2][:, (i % 2) * P : (i % 2 + 1) * P].bitcast(FP8X4),
+                    lhsT_scale=w2_scales[i // 2][:, (i % 2) * P : (i % 2 + 1) * P],
+                    rhs=z_codes[h][:].bitcast(FP8X4),
+                    rhs_scale=z_scales[h][:],
                     start=True,
                     stop=True,
                 )
-            result = sb(f"result{c}_{tiles[0]}", [P, len(tiles), count * CHUNK], F32)
+            result = sb(f"result{h}_{tiles[0]}", [P, len(tiles), HALF], F32)
             copy(result[:], acc[:])
-            queue.dma_start(out_view[:, tiles[0] : tiles[-1] + 1, tokens(c, count)], result[:])
+            queue.dma_start(out_view[:, tiles[0] : tiles[-1] + 1, h * HALF : (h + 1) * HALF], result[:])
 
-        for g in range(PASSES):
-            for c in range(EARLY):
-                for t in range(PACK):
-                    first_product_pass(c, t, g)
-        round_w2_on_gpsimd(0)
+        w2_bf = [sb("w2_bf0", [P, N // 2 * PACK], BF16)]
+        nc.gpsimd.tensor_scalar(
+            w2_bf[0][:].rearrange("p (c j) -> p c j", j=PACK),
+            w2_raw[0][:].rearrange("p j c -> p c j"),
+            1.0,
+            0.0,
+            ALU.mult,
+            ALU.add,
+        )
         negative_part(0)
         positive_part(1)
         negative_part(2)
         positive_part(0)
-        y.append(psum_y.tile([P, PACK, CHUNK], F32, name="y0"))
-        for t in range(PACK):
-            for g in range(PASSES):
-                first_product_pass(3, t, g)
+        y.append(psum.tile([P, PACK, CHUNK], F32, name="bank0"))
+        for g in range(PASSES):
+            for t in range(PACK):
+                first_product_pass(LAST, t, g)
         negative_part(1)
-        round_w2(1, 0, 2 * P, nc.scalar.copy)
-        positive_part(3)
         positive_part(2)
-        quantize_w2(0)
+        w2_bf.append(sb("woven2", [P, N // 2 * PACK], BF16))
+        nc.scalar.copy(
+            w2_bf[1][:].rearrange("p (c i j) -> p c j i", i=4, j=PACK),
+            w2_raw[1][:].rearrange("p j (c i) -> p c j i", i=4),
+        )
         join(0)
         join(1)
-        quantize_z(0)
-        quantize_z(1)
-        second_product(0, 2, [0, 1], psum_o, "acc", nc.scalar.copy, nc.sync)
-        quantize_w2(1)
-        second_product(0, 2, [2, 3], psum_o, "acc", nc.scalar.copy, nc.sync)
-        below.append(sb("z_bf0", [P, CHUNK * PACK], BF16)[:])
-        negative_part(3)
+        w2_codes = [sb("woven1", [P, N // 2], U32), sb("w2_codes1", [P, N // 2], U32)]
+        quantize_w2(0)
+        nc.vector.quantize_mx(out=z_codes[0][:].bitcast(FP8X4), scales=z_scales[0][:], in_=z_early[:])
+        second_product(0, [0, 1], "bank3", nc.scalar.copy, nc.sync)
         join(2)
-        join(3)
-        quantize_z(2)
-        quantize_z(3)
-        second_product(2, 2, [0], psum_o, "acc", nc.vector.tensor_copy, nc.sync)
-        second_product(2, 2, [1], psum_o, "acc", nc.scalar.copy, nc.scalar)
-        second_product(2, 2, [2], psum_y, "y1", nc.vector.tensor_copy, nc.sync)
-        second_product(2, 2, [3], psum_y, "y2", nc.scalar.copy, nc.scalar)
+        below.append(sb("w2_bf0", [P, CHUNK * PACK], BF16))
+        negative_part(LAST)
+        quantize_w2(1)
+        second_product(0, [2, 3], "bank4", nc.scalar.copy, nc.sync)
+        nc.vector.scalar_tensor_tensor(
+            out=by_token(z_bf[LAST]),
+            in0=sums(LAST),
+            scalar=0.0,
+            in1=by_token(below[LAST][:]),
+            op0=ALU.max,
+            op1=ALU.add,
+        )
+        for c in (2, 3):
+            nc.vector.quantize_mx(
+                out=z_codes[1][:, tokens(c - 2)].bitcast(FP8X4), scales=z_scales[1][:, tokens(c - 2)], in_=z_bf[c]
+            )
+        second_product(1, [0], "bank5", nc.vector.tensor_copy, nc.sync)
+        second_product(1, [1], "bank6", nc.scalar.copy, nc.scalar)
+        second_product(1, [2], "bank7", nc.vector.tensor_copy, nc.sync)
+        second_product(1, [3], "bank1", nc.scalar.copy, nc.scalar)

@@ -55,13 +55,16 @@ def tile_picked_prelu8_none_p_kernel(tc, x_words, x_scales, w1, slope, w2, offs,
         nc.sync.dma_start(slope_rows[0][:], slope_view[:, 0, :])
         nc.sync.dma_start(task_list[:], task)
         nc.sync.dma_start(slope_rows[1][:], slope_view[:, 1, :])
-        nc.sync.dma_start(offs_list[:], offs)
-        for g in range(PASSES):
-            nc.sync.dma_start(scale_table[4 * g : P : 8, :].bitcast(I32), x_scales[g].bitcast(I32))
+        for q in range(4):
+            nc.gpsimd.dma_start(
+                scale_table[32 * q : 32 * q + 4 * PASSES, :].bitcast(I32),
+                x_scales[:, 4 * q : 4 * q + 4, :].bitcast(I32),
+            )
         for t in range(2, PACK):
             nc.sync.dma_start(slope_rows[t][:], slope_view[:, t, :])
-        for g in range(PASSES):
-            nc.sync.dma_start(w1_raw[g][:], w1_view[g])
+        nc.sync.dma_start(w1_raw[0][:], w1_view[0])
+        nc.sync.dma_start(offs_list[:], offs)
+        nc.sync.dma_start(w1_raw[1][:], w1_view[1])
         for g in range(PASSES):
             nc.sync.dma_start(x_table[g][:], x_words[g].rearrange("p n t -> p (n t)").bitcast(I32))
         for h in range(2):
@@ -75,20 +78,8 @@ def tile_picked_prelu8_none_p_kernel(tc, x_words, x_scales, w1, slope, w2, offs,
                     picked_slope[h][:, t, :], slope_rows[t][:].indirect(task_list[:, entries(h * HALF, HALF)])
                 )
 
-        picked_scales = sb("picked_scales", [P, S], U8)
-        x_plane = sb("x_plane", [P, S], U8)
-        pick_slopes(0)
-        pick_slopes(1)
-        nc.vector.tensor_copy(picked_scales[:], scale_table[:].indirect(offs_list[:]))
-        pick_slopes(2)
-        nc.vector.tensor_copy(x_plane[:].bitcast(I32), picked_scales[:].bitcast(I32))
-        for g in range(PASSES):
-            for i in range(1, 4):
-                nc.gpsimd.dma_start(
-                    x_plane[4 * g + i : P : 32, :].bitcast(I32),
-                    picked_scales[4 * g + 8 * i : P : 32, :].bitcast(I32),
-                )
-        pick_slopes(3)
+        for t in range(PACK):
+            pick_slopes(t)
 
         woven = [sb(f"woven{c}", [P, CHUNK, PACK], F32) for c in range(CHUNKS)]
 
@@ -105,11 +96,13 @@ def tile_picked_prelu8_none_p_kernel(tc, x_words, x_scales, w1, slope, w2, offs,
                 w1_raw[g][:].rearrange("p j (m a b) -> p a m j b", a=2, b=2),
             )
         for c in range(CHUNKS):
-            weave(c, nc.vector.tensor_copy if c < 4 else nc.scalar.copy)
+            weave(c, nc.vector.tensor_copy if c < 2 else nc.scalar.copy)
 
         w1_scales = [sb(f"w1_scales{g}", [P, H], U8) for g in range(PASSES)]
         w1_codes = [sb("w1_codes0", [P, H], U32)]
         nc.vector.quantize_mx(out=w1_codes[0][:].bitcast(FP8X4), scales=w1_scales[0][:], in_=w1_bf[0][:])
+        x_plane = sb("w1_bf0", [P, S], U8)
+        nc.vector.tensor_copy(x_plane[:], scale_table[:].indirect(offs_list[:]))
         x_first = [sb(f"x_first{h}", [P, HALF], U32) for h in range(2)]
         for h in range(2):
             nc.vector.tensor_copy(

@@ -96,7 +96,7 @@ def tile_picked_prelu8_none_p_kernel(tc, x_words, x_scales, w1, slope, w2, offs,
                 w1_raw[g][:].rearrange("p j (m a b) -> p a m j b", a=2, b=2),
             )
         for c in range(CHUNKS):
-            weave(c, nc.vector.tensor_copy if c < 2 else nc.scalar.copy)
+            weave(c, nc.vector.tensor_copy if c < 4 else nc.scalar.copy)
 
         w1_scales = [sb(f"w1_scales{g}", [P, H], U8) for g in range(PASSES)]
         w1_codes = [sb("w1_codes0", [P, H], U32)]

@@ -13,6 +13,7 @@ U16 = mybir.dt.uint16
 U8 = mybir.dt.uint8
 FP8X4 = mybir.dt.float8_e4m3fn_x4
 ALU = mybir.AluOpType
+COPY = mybir.ActivationFunctionType.Copy
 RELU = mybir.ActivationFunctionType.Relu
 
 P = 128
@@ -45,26 +46,25 @@ def tile_picked_prelu8_none_p_kernel(tc, x_words, x_scales, w1, slope, w2, offs,
         w1_raw = [sb(f"w1_raw{g}", [P, PACK, H], F32) for g in range(PASSES)]
         w2_raw = [sb(f"w2_raw{h}", [P, PACK, N // 2], F32) for h in range(2)]
         x_table = [sb(f"x_table{g}", [P, T], I32) for g in range(PASSES)]
-        scale_table = sb("scale_table", [P, T], U8)
+        scale_table = sb("scale_table", [P, PASSES * T], U8)
 
-        nc.vector.memset(scale_table[:].bitcast(I32), 0)
+        nc.gpsimd.memset(scale_table[:, :T].bitcast(I32), 0)
+        nc.vector.memset(scale_table[:, T:].bitcast(I32), 0)
 
         slope_view = slope.rearrange("(p t) u -> p t u", t=PACK)
         w1_view = w1.rearrange("(g p j) c -> g p j c", p=P, j=PACK)
         w2_view = w2.rearrange("(p j) c -> p j c", j=PACK)
         nc.sync.dma_start(slope_rows[0][:], slope_view[:, 0, :])
         nc.sync.dma_start(task_list[:], task)
-        nc.sync.dma_start(slope_rows[1][:], slope_view[:, 1, :])
-        for q in range(4):
-            nc.gpsimd.dma_start(
-                scale_table[32 * q : 32 * q + 4 * PASSES, :].bitcast(I32),
-                x_scales[:, 4 * q : 4 * q + 4, :].bitcast(I32),
-            )
-        for t in range(2, PACK):
-            nc.sync.dma_start(slope_rows[t][:], slope_view[:, t, :])
-        nc.sync.dma_start(w1_raw[0][:], w1_view[0])
         nc.sync.dma_start(offs_list[:], offs)
-        nc.sync.dma_start(w1_raw[1][:], w1_view[1])
+        nc.sync.dma_start(
+            scale_table[0:P:8, :].bitcast(I32).rearrange("r (g n) -> r g n", g=PASSES),
+            x_scales.bitcast(I32).rearrange("g r n -> r g n"),
+        )
+        for t in range(1, PACK):
+            nc.sync.dma_start(slope_rows[t][:], slope_view[:, t, :])
+        for g in range(PASSES):
+            nc.sync.dma_start(w1_raw[g][:], w1_view[g])
         for g in range(PASSES):
             nc.sync.dma_start(x_table[g][:], x_words[g].rearrange("p n t -> p (n t)").bitcast(I32))
         for h in range(2):
@@ -72,14 +72,29 @@ def tile_picked_prelu8_none_p_kernel(tc, x_words, x_scales, w1, slope, w2, offs,
 
         picked_slope = [sb(f"picked_slope{h}", [P, PACK, HALF], F32) for h in range(2)]
 
-        def pick_slopes(t):
-            for h in range(2):
-                nc.vector.tensor_copy(
-                    picked_slope[h][:, t, :], slope_rows[t][:].indirect(task_list[:, entries(h * HALF, HALF)])
-                )
+        def pick_slopes(t, h):
+            looked_up = slope_rows[t][:].indirect(task_list[:, entries(h * HALF, HALF)])
+            if t == 1:
+                nc.scalar.activation(out=picked_slope[h][:, t, :], in_=looked_up, func=COPY)
+            else:
+                nc.vector.tensor_copy(picked_slope[h][:, t, :], looked_up)
 
-        for t in range(PACK):
-            pick_slopes(t)
+        picked_scales = sb("picked_scales", [P, PASSES * S], U8)
+        x_plane = sb("x_plane", [P, PASSES * S], U8)
+        for t in range(2):
+            for h in range(2):
+                pick_slopes(t, h)
+        for g in range(PASSES):
+            nc.vector.tensor_copy(
+                picked_scales[:, g * S : (g + 1) * S], scale_table[:, g * T : (g + 1) * T].indirect(offs_list[:])
+            )
+        pick_slopes(2, 0)
+        nc.vector.tensor_copy(x_plane[:].bitcast(I32), picked_scales[:].bitcast(I32))
+        for i in range(1, 4):
+            nc.scalar.dma_start(x_plane[i:P:32, :].bitcast(I32), picked_scales[8 * i : P : 32, :].bitcast(I32))
+        pick_slopes(2, 1)
+        for h in range(2):
+            pick_slopes(3, h)
 
         woven = [sb(f"woven{c}", [P, CHUNK, PACK], F32) for c in range(CHUNKS)]
 
@@ -101,8 +116,6 @@ def tile_picked_prelu8_none_p_kernel(tc, x_words, x_scales, w1, slope, w2, offs,
         w1_scales = [sb(f"w1_scales{g}", [P, H], U8) for g in range(PASSES)]
         w1_codes = [sb("w1_codes0", [P, H], U32)]
         nc.vector.quantize_mx(out=w1_codes[0][:].bitcast(FP8X4), scales=w1_scales[0][:], in_=w1_bf[0][:])
-        x_plane = sb("w1_bf0", [P, S], U8)
-        nc.vector.tensor_copy(x_plane[:], scale_table[:].indirect(offs_list[:]))
         x_first = [sb(f"x_first{h}", [P, HALF], U32) for h in range(2)]
         for h in range(2):
             nc.vector.tensor_copy(
@@ -126,7 +139,7 @@ def tile_picked_prelu8_none_p_kernel(tc, x_words, x_scales, w1, slope, w2, offs,
                 lhsT=w1_codes[g][:, t * P : (t + 1) * P].bitcast(FP8X4),
                 lhsT_scale=w1_scales[g][:, t * P : (t + 1) * P],
                 rhs=moving[g].bitcast(FP8X4),
-                rhs_scale=x_plane[4 * g : P, tokens(c)],
+                rhs_scale=x_plane[:, tokens(g * CHUNKS + c)],
                 start=(g == 0 and t == 0),
                 stop=(g == PASSES - 1 and t == PACK - 1),
             )

@@ -56,12 +56,13 @@ def tile_picked_prelu8_none_p_kernel(tc, x_words, x_scales, w1, slope, w2, offs,
         w2_view = w2.rearrange("(p j) c -> p j c", j=PACK)
         nc.sync.dma_start(slope_rows[0][:], slope_view[:, 0, :])
         nc.sync.dma_start(task_list[:], task)
+        nc.sync.dma_start(slope_rows[1][:], slope_view[:, 1, :])
         nc.sync.dma_start(offs_list[:], offs)
         nc.sync.dma_start(
             scale_table[0:P:8, :].bitcast(I32).rearrange("r (g n) -> r g n", g=PASSES),
             x_scales.bitcast(I32).rearrange("g r n -> r g n"),
         )
-        for t in range(1, PACK):
+        for t in range(2, PACK):
             nc.sync.dma_start(slope_rows[t][:], slope_view[:, t, :])
         for g in range(PASSES):
             nc.sync.dma_start(w1_raw[g][:], w1_view[g])

@@ -124,17 +124,21 @@ def tile_picked_prelu8_none_p_kernel(tc, x_words, x_scales, w1, slope, w2, offs,
             )
         w1_codes.append(sb("x_table0", [P, H], U32))
         nc.vector.quantize_mx(out=w1_codes[1][:].bitcast(FP8X4), scales=w1_scales[1][:], in_=w1_bf[1][:])
-        pieces = [(0, 1), (1, 1), (2, 2)]
-        x_second = [sb(f"x_second{c}", [P, count * CHUNK], U32) for c, count in pieces]
-        for picked, (c, count) in zip(x_second, pieces):
+        x_second = []
+
+        def pick_second(c, name):
+            x_second.append(sb(name, [P, CHUNK], U32))
             nc.vector.tensor_copy(
-                picked[:], x_table[1][:].bitcast(U32).indirect(offs_list[:, entries(c * CHUNK, count * CHUNK)])
+                x_second[c][:], x_table[1][:].bitcast(U32).indirect(offs_list[:, entries(c * CHUNK, CHUNK)])
             )
+
+        for c in range(LAST):
+            pick_second(c, f"x_second{c}")
 
         y = [psum.tile([P, PACK, CHUNK], F32, name=f"bank{c}") for c in range(LAST)]
 
         def first_product_pass(c, t, g):
-            moving = [x_first[c // 2][:, tokens(c % 2)], x_second[min(c, 2)][:, tokens(max(c - 2, 0))]]
+            moving = [x_first[c // 2][:, tokens(c % 2)], x_second[c][:]]
             nc.tensor.matmul_mx(
                 out=y[c][:, t, :],
                 lhsT=w1_codes[g][:, t * P : (t + 1) * P].bitcast(FP8X4),
@@ -209,6 +213,7 @@ def tile_picked_prelu8_none_p_kernel(tc, x_words, x_scales, w1, slope, w2, offs,
         positive_part(1)
         negative_part(2)
         positive_part(0)
+        pick_second(LAST, "x_second2")
         y.append(psum.tile([P, PACK, CHUNK], F32, name="bank0"))
         for g in range(PASSES):
             for t in range(PACK):
@@ -226,24 +231,82 @@ def tile_picked_prelu8_none_p_kernel(tc, x_words, x_scales, w1, slope, w2, offs,
         quantize_w2(0)
         nc.vector.quantize_mx(out=z_codes[0][:].bitcast(FP8X4), scales=z_scales[0][:], in_=z_early[:])
         second_product(0, [0, 1], "bank3", nc.scalar.copy, nc.sync)
-        join(2)
-        below.append(sb("w2_bf0", [P, CHUNK * PACK], BF16))
-        negative_part(LAST)
-        quantize_w2(1)
-        second_product(0, [2, 3], "bank4", nc.scalar.copy, nc.sync)
-        nc.vector.scalar_tensor_tensor(
-            out=by_token(z_bf[LAST]),
-            in0=sums(LAST),
-            scalar=0.0,
-            in1=by_token(below[LAST][:]),
-            op0=ALU.max,
-            op1=ALU.add,
-        )
-        for c in (2, 3):
+
+        def quantize_z(c):
             nc.vector.quantize_mx(
                 out=z_codes[1][:, tokens(c - 2)].bitcast(FP8X4), scales=z_scales[1][:, tokens(c - 2)], in_=z_bf[c]
             )
-        second_product(1, [0], "bank5", nc.vector.tensor_copy, nc.sync)
-        second_product(1, [1], "bank6", nc.scalar.copy, nc.scalar)
-        second_product(1, [2], "bank7", nc.vector.tensor_copy, nc.sync)
-        second_product(1, [3], "bank1", nc.scalar.copy, nc.scalar)
+
+        def late_product(c, tiles, bank, copy, queue):
+            acc = psum.tile([P, len(tiles), CHUNK], F32, name=bank)
+            for n, i in enumerate(tiles):
+                nc.tensor.matmul_mx(
+                    out=acc[:, n, :],
+                    lhsT=w2_codes[i // 2][:, (i % 2) * P : (i % 2 + 1) * P].bitcast(FP8X4),
+                    lhsT_scale=w2_scales[i // 2][:, (i % 2) * P : (i % 2 + 1) * P],
+                    rhs=z_codes[1][:, tokens(c - 2)].bitcast(FP8X4),
+                    rhs_scale=z_scales[1][:, tokens(c - 2)],
+                    start=True,
+                    stop=True,
+                )
+            result = sb(f"late_result{c}_{tiles[0]}", [P, len(tiles), CHUNK], F32)
+            copy(result[:], acc[:])
+            queue.dma_start(out_view[:, tiles[0] : tiles[-1] + 1, tokens(c)], result[:])
+
+        def late_pass(acc, i, c):
+            nc.tensor.matmul_mx(
+                out=acc,
+                lhsT=w2_codes[i // 2][:, (i % 2) * P : (i % 2 + 1) * P].bitcast(FP8X4),
+                lhsT_scale=w2_scales[i // 2][:, (i % 2) * P : (i % 2 + 1) * P],
+                rhs=z_codes[1][:, tokens(c - 2)].bitcast(FP8X4),
+                rhs_scale=z_scales[1][:, tokens(c - 2)],
+                start=True,
+                stop=True,
+            )
+
+        PART = CHUNK // 2
+        last_below = []
+
+        def part(u):
+            return slice(u * PART, (u + 1) * PART)
+
+        def last_negative(u, name):
+            last_below.append(sb(name, [P, PART * PACK], BF16))
+            nc.vector.scalar_tensor_tensor(
+                out=by_token(last_below[u][:]),
+                in0=sums(LAST)[:, part(u), :],
+                scalar=0.0,
+                in1=woven[LAST][:, part(u), :],
+                op0=ALU.min,
+                op1=ALU.mult,
+            )
+
+        def last_sum(u):
+            nc.vector.scalar_tensor_tensor(
+                out=by_token(z_bf[LAST])[:, part(u), :],
+                in0=sums(LAST)[:, part(u), :],
+                scalar=0.0,
+                in1=by_token(last_below[u][:]),
+                op0=ALU.max,
+                op1=ALU.add,
+            )
+
+        join(2)
+        last_negative(0, "w2_bf0")
+        quantize_z(2)
+        late_product(2, [0, 1], "bank5", nc.scalar.copy, nc.sync)
+        quantize_w2(1)
+        second_product(0, [2, 3], "bank4", nc.scalar.copy, nc.sync)
+        single = [psum.tile([P, CHUNK], F32, name=bank) for bank in ("bank6", "bank7")]
+        for i in range(2):
+            late_pass(single[i][:], 2 + i, 2)
+        last_negative(1, "above2")
+        for u in range(2):
+            last_sum(u)
+        early_result = sb("early_result", [P, 2, CHUNK], F32)
+        nc.vector.tensor_copy(early_result[:, 0, :], single[0][:])
+        nc.scalar.copy(early_result[:, 1, :], single[1][:])
+        nc.sync.dma_start(out_view[:, 2:4, tokens(2)], early_result[:])
+        quantize_z(LAST)
+        late_product(LAST, [0, 1], "bank1", nc.vector.tensor_copy, nc.sync)
+        late_product(LAST, [2, 3], "bank2", nc.scalar.copy, nc.scalar)

@@ -75,27 +75,25 @@ def tile_picked_prelu8_none_p_kernel(tc, x_words, x_scales, w1, slope, w2, offs,
 
         def pick_slopes(t, h):
             looked_up = slope_rows[t][:].indirect(task_list[:, entries(h * HALF, HALF)])
-            if t == 1:
+            if t in (1, 2):
                 nc.scalar.activation(out=picked_slope[h][:, t, :], in_=looked_up, func=COPY)
             else:
                 nc.vector.tensor_copy(picked_slope[h][:, t, :], looked_up)
 
         picked_scales = sb("picked_scales", [P, PASSES * S], U8)
         x_plane = sb("x_plane", [P, PASSES * S], U8)
-        for t in range(2):
+        for t in range(3):
             for h in range(2):
                 pick_slopes(t, h)
         for g in range(PASSES):
             nc.vector.tensor_copy(
                 picked_scales[:, g * S : (g + 1) * S], scale_table[:, g * T : (g + 1) * T].indirect(offs_list[:])
             )
-        pick_slopes(2, 0)
+        pick_slopes(3, 0)
         nc.vector.tensor_copy(x_plane[:].bitcast(I32), picked_scales[:].bitcast(I32))
         for i in range(1, 4):
             nc.scalar.dma_start(x_plane[i:P:32, :].bitcast(I32), picked_scales[8 * i : P : 32, :].bitcast(I32))
-        pick_slopes(2, 1)
-        for h in range(2):
-            pick_slopes(3, h)
+        pick_slopes(3, 1)
 
         woven = [sb(f"woven{c}", [P, CHUNK, PACK], F32) for c in range(CHUNKS)]
 

from contextlib import ExitStack

import concourse.mybir as mybir

K, T, S, N, H, U = 1024, 2048, 512, 512, 512, 512
FLOPS = 2 * K * H * S + 2 * H * N * S

F32 = mybir.dt.float32
BF16 = mybir.dt.bfloat16
I32 = mybir.dt.int32
U32 = mybir.dt.uint32
U16 = mybir.dt.uint16
U8 = mybir.dt.uint8
FP8X4 = mybir.dt.float8_e4m3fn_x4
ALU = mybir.AluOpType
COPY = mybir.ActivationFunctionType.Copy
RELU = mybir.ActivationFunctionType.Relu

P = 128
PACK = 4
PASSES = K // (P * PACK)
HALF = S // 2
CHUNK = 128
CHUNKS = S // CHUNK
LAST = CHUNKS - 1


def tile_picked_prelu8_none_p_kernel(tc, x_words, x_scales, w1, slope, w2, offs, task, out):
    nc = tc.nc
    with ExitStack() as ctx:
        keep = ctx.enter_context(tc.tile_pool(name="keep", bufs=1))
        psum = ctx.enter_context(tc.psum_pool(name="psum", bufs=1))

        def sb(name, shape, dtype):
            return keep.tile(shape, dtype, name=name, align_bytes=64)

        def entries(first, count):
            return slice(first // 16, (first + count) // 16)

        def tokens(c, count=1):
            return slice(c * CHUNK, (c + count) * CHUNK)

        task_list = sb("task_list", [P, S // 16], U16)
        offs_list = sb("offs_list", [P, S // 16], U16)
        slope_rows = [sb(f"slope_rows{t}", [P, U], F32) for t in range(PACK)]
        w1_raw = [sb(f"w1_raw{g}", [P, PACK, H], F32) for g in range(PASSES)]
        w2_raw = [sb(f"w2_raw{h}", [P, PACK, N // 2], F32) for h in range(2)]
        x_table = [sb(f"x_table{g}", [P, T], I32) for g in range(PASSES)]
        scale_table = sb("scale_table", [P, PASSES * T], U8)

        nc.gpsimd.memset(scale_table[:, :T].bitcast(I32), 0)
        nc.vector.memset(scale_table[:, T:].bitcast(I32), 0)

        slope_view = slope.rearrange("(p t) u -> p t u", t=PACK)
        w1_view = w1.rearrange("(g p j) c -> g p j c", p=P, j=PACK)
        w2_view = w2.rearrange("(p j) c -> p j c", j=PACK)
        nc.sync.dma_start(slope_rows[0][:], slope_view[:, 0, :])
        nc.sync.dma_start(task_list[:], task)
        nc.sync.dma_start(slope_rows[1][:], slope_view[:, 1, :])
        nc.sync.dma_start(offs_list[:], offs)
        nc.sync.dma_start(
            scale_table[0:P:8, :].bitcast(I32).rearrange("r (g n) -> r g n", g=PASSES),
            x_scales.bitcast(I32).rearrange("g r n -> r g n"),
        )
        for t in range(2, PACK):
            nc.sync.dma_start(slope_rows[t][:], slope_view[:, t, :])
        for g in range(PASSES):
            nc.sync.dma_start(w1_raw[g][:], w1_view[g])
        for g in range(PASSES):
            nc.sync.dma_start(x_table[g][:], x_words[g].rearrange("p n t -> p (n t)").bitcast(I32))
        for h in range(2):
            nc.sync.dma_start(w2_raw[h][:], w2_view[:, :, h * (N // 2) : (h + 1) * (N // 2)])

        picked_slope = [sb(f"picked_slope{h}", [P, PACK, HALF], F32) for h in range(2)]

        def pick_slopes(t, h):
            looked_up = slope_rows[t][:].indirect(task_list[:, entries(h * HALF, HALF)])
            if t in (1, 2):
                nc.scalar.activation(out=picked_slope[h][:, t, :], in_=looked_up, func=COPY)
            else:
                nc.vector.tensor_copy(picked_slope[h][:, t, :], looked_up)

        picked_scales = sb("picked_scales", [P, PASSES * S], U8)
        x_plane = sb("x_plane", [P, PASSES * S], U8)
        for t in range(3):
            for h in range(2):
                pick_slopes(t, h)
        for g in range(PASSES):
            nc.vector.tensor_copy(
                picked_scales[:, g * S : (g + 1) * S], scale_table[:, g * T : (g + 1) * T].indirect(offs_list[:])
            )
        pick_slopes(3, 0)
        nc.vector.tensor_copy(x_plane[:].bitcast(I32), picked_scales[:].bitcast(I32))
        for i in range(1, 4):
            nc.scalar.dma_start(x_plane[i:P:32, :].bitcast(I32), picked_scales[8 * i : P : 32, :].bitcast(I32))
        pick_slopes(3, 1)

        woven = [sb(f"woven{c}", [P, CHUNK, PACK], F32) for c in range(CHUNKS)]

        def weave(c, copy):
            copy(
                woven[c][:].rearrange("p (c i) t -> p c t i", i=2),
                picked_slope[c // 2][:, :, tokens(c % 2)].rearrange("p t (c i) -> p c t i", i=2),
            )

        w1_bf = [sb(f"w1_bf{g}", [P, H * PACK], BF16) for g in range(PASSES)]
        for g in range(PASSES):
            nc.scalar.copy(
                w1_bf[g][:].rearrange("p (a b m j) -> p a m j b", a=2, b=2, j=PACK),
                w1_raw[g][:].rearrange("p j (m a b) -> p a m j b", a=2, b=2),
            )
        for c in range(CHUNKS):
            weave(c, nc.vector.tensor_copy if c < 4 else nc.scalar.copy)

        w1_scales = [sb(f"w1_scales{g}", [P, H], U8) for g in range(PASSES)]
        w1_codes = [sb("w1_codes0", [P, H], U32)]
        nc.vector.quantize_mx(out=w1_codes[0][:].bitcast(FP8X4), scales=w1_scales[0][:], in_=w1_bf[0][:])
        x_first = [sb(f"x_first{h}", [P, HALF], U32) for h in range(2)]
        for h in range(2):
            nc.vector.tensor_copy(
                x_first[h][:], x_table[0][:].bitcast(U32).indirect(offs_list[:, entries(h * HALF, HALF)])
            )
        w1_codes.append(sb("x_table0", [P, H], U32))
        nc.vector.quantize_mx(out=w1_codes[1][:].bitcast(FP8X4), scales=w1_scales[1][:], in_=w1_bf[1][:])
        x_second = []

        def pick_second(c, name):
            x_second.append(sb(name, [P, CHUNK], U32))
            nc.vector.tensor_copy(
                x_second[c][:], x_table[1][:].bitcast(U32).indirect(offs_list[:, entries(c * CHUNK, CHUNK)])
            )

        for c in range(LAST):
            pick_second(c, f"x_second{c}")

        y = [psum.tile([P, PACK, CHUNK], F32, name=f"bank{c}") for c in range(LAST)]

        def first_product_pass(c, t, g):
            moving = [x_first[c // 2][:, tokens(c % 2)], x_second[c][:]]
            nc.tensor.matmul_mx(
                out=y[c][:, t, :],
                lhsT=w1_codes[g][:, t * P : (t + 1) * P].bitcast(FP8X4),
                lhsT_scale=w1_scales[g][:, t * P : (t + 1) * P],
                rhs=moving[g].bitcast(FP8X4),
                rhs_scale=x_plane[:, tokens(g * CHUNKS + c)],
                start=(g == 0 and t == 0),
                stop=(g == PASSES - 1 and t == PACK - 1),
            )

        for g in range(PASSES):
            for c in range(LAST):
                for t in range(PACK):
                    first_product_pass(c, t, g)

        def by_token(ap):
            return ap.rearrange("p (s t) -> p s t", t=PACK)

        def sums(c):
            return y[c][:].rearrange("p t s -> p s t")

        below = [sb(f"below{c}", [P, CHUNK * PACK], BF16) for c in range(LAST)]
        above = [sb(f"above{c}", [P, CHUNK * PACK], BF16) for c in range(LAST)]
        z_early = sb("z_early", [P, 2 * CHUNK * PACK], BF16)
        z_bf = [z_early[:, : CHUNK * PACK], z_early[:, CHUNK * PACK :]]
        z_bf = z_bf + [sb(f"z_late{c}", [P, CHUNK * PACK], BF16)[:] for c in (2, 3)]
        z_codes = [sb(f"z_codes{h}", [P, HALF], U32) for h in range(2)]
        z_scales = [sb(f"z_scales{h}", [P, HALF], U8) for h in range(2)]
        w2_scales = [sb(f"w2_scales{h}", [P, N // 2], U8) for h in range(2)]
        out_view = out.rearrange("(i p) s -> p i s", p=P)

        def negative_part(c):
            nc.vector.scalar_tensor_tensor(
                out=by_token(below[c][:]), in0=sums(c), scalar=0.0, in1=woven[c][:], op0=ALU.min, op1=ALU.mult
            )

        def positive_part(c):
            nc.scalar.activation(out=by_token(above[c][:]), in_=sums(c), func=RELU)

        def join(c):
            nc.vector.tensor_tensor(z_bf[c], below[c][:], above[c][:], ALU.add)

        def quantize_w2(h):
            nc.vector.quantize_mx(out=w2_codes[h][:].bitcast(FP8X4), scales=w2_scales[h][:], in_=w2_bf[h][:])

        def second_product(h, tiles, bank, copy, queue):
            acc = psum.tile([P, len(tiles), HALF], F32, name=bank)
            for n, i in enumerate(tiles):
                nc.tensor.matmul_mx(
                    out=acc[:, n, :],
                    lhsT=w2_codes[i // 2][:, (i % 2) * P : (i % 2 + 1) * P].bitcast(FP8X4),
                    lhsT_scale=w2_scales[i // 2][:, (i % 2) * P : (i % 2 + 1) * P],
                    rhs=z_codes[h][:].bitcast(FP8X4),
                    rhs_scale=z_scales[h][:],
                    start=True,
                    stop=True,
                )
            result = sb(f"result{h}_{tiles[0]}", [P, len(tiles), HALF], F32)
            copy(result[:], acc[:])
            queue.dma_start(out_view[:, tiles[0] : tiles[-1] + 1, h * HALF : (h + 1) * HALF], result[:])

        w2_bf = [sb("w2_bf0", [P, N // 2 * PACK], BF16)]
        nc.gpsimd.tensor_scalar(
            w2_bf[0][:].rearrange("p (c j) -> p c j", j=PACK),
            w2_raw[0][:].rearrange("p j c -> p c j"),
            1.0,
            0.0,
            ALU.mult,
            ALU.add,
        )
        negative_part(0)
        positive_part(1)
        negative_part(2)
        positive_part(0)
        pick_second(LAST, "x_second2")
        y.append(psum.tile([P, PACK, CHUNK], F32, name="bank0"))
        for g in range(PASSES):
            for t in range(PACK):
                first_product_pass(LAST, t, g)
        negative_part(1)
        positive_part(2)
        w2_bf.append(sb("woven2", [P, N // 2 * PACK], BF16))
        nc.scalar.copy(
            w2_bf[1][:].rearrange("p (c i j) -> p c j i", i=4, j=PACK),
            w2_raw[1][:].rearrange("p j (c i) -> p c j i", i=4),
        )
        join(0)
        join(1)
        w2_codes = [sb("woven1", [P, N // 2], U32), sb("w2_codes1", [P, N // 2], U32)]
        quantize_w2(0)
        nc.vector.quantize_mx(out=z_codes[0][:].bitcast(FP8X4), scales=z_scales[0][:], in_=z_early[:])
        second_product(0, [0, 1], "bank3", nc.scalar.copy, nc.sync)

        def quantize_z(c):
            nc.vector.quantize_mx(
                out=z_codes[1][:, tokens(c - 2)].bitcast(FP8X4), scales=z_scales[1][:, tokens(c - 2)], in_=z_bf[c]
            )

        def late_product(c, tiles, bank, copy, queue):
            acc = psum.tile([P, len(tiles), CHUNK], F32, name=bank)
            for n, i in enumerate(tiles):
                nc.tensor.matmul_mx(
                    out=acc[:, n, :],
                    lhsT=w2_codes[i // 2][:, (i % 2) * P : (i % 2 + 1) * P].bitcast(FP8X4),
                    lhsT_scale=w2_scales[i // 2][:, (i % 2) * P : (i % 2 + 1) * P],
                    rhs=z_codes[1][:, tokens(c - 2)].bitcast(FP8X4),
                    rhs_scale=z_scales[1][:, tokens(c - 2)],
                    start=True,
                    stop=True,
                )
            result = sb(f"late_result{c}_{tiles[0]}", [P, len(tiles), CHUNK], F32)
            copy(result[:], acc[:])
            queue.dma_start(out_view[:, tiles[0] : tiles[-1] + 1, tokens(c)], result[:])

        def late_pass(acc, i, c):
            nc.tensor.matmul_mx(
                out=acc,
                lhsT=w2_codes[i // 2][:, (i % 2) * P : (i % 2 + 1) * P].bitcast(FP8X4),
                lhsT_scale=w2_scales[i // 2][:, (i % 2) * P : (i % 2 + 1) * P],
                rhs=z_codes[1][:, tokens(c - 2)].bitcast(FP8X4),
                rhs_scale=z_scales[1][:, tokens(c - 2)],
                start=True,
                stop=True,
            )

        PART = CHUNK // 2
        last_below = []

        def part(u):
            return slice(u * PART, (u + 1) * PART)

        def last_negative(u, name):
            last_below.append(sb(name, [P, PART * PACK], BF16))
            nc.vector.scalar_tensor_tensor(
                out=by_token(last_below[u][:]),
                in0=sums(LAST)[:, part(u), :],
                scalar=0.0,
                in1=woven[LAST][:, part(u), :],
                op0=ALU.min,
                op1=ALU.mult,
            )

        def last_sum(u):
            nc.vector.scalar_tensor_tensor(
                out=by_token(z_bf[LAST])[:, part(u), :],
                in0=sums(LAST)[:, part(u), :],
                scalar=0.0,
                in1=by_token(last_below[u][:]),
                op0=ALU.max,
                op1=ALU.add,
            )

        join(2)
        last_negative(0, "w2_bf0")
        quantize_z(2)
        late_product(2, [0, 1], "bank5", nc.scalar.copy, nc.sync)
        quantize_w2(1)
        second_product(0, [2, 3], "bank4", nc.scalar.copy, nc.sync)
        single = [psum.tile([P, CHUNK], F32, name=bank) for bank in ("bank6", "bank7")]
        for i in range(2):
            late_pass(single[i][:], 2 + i, 2)
        last_negative(1, "above2")
        for u in range(2):
            last_sum(u)
        early_result = sb("early_result", [P, 2, CHUNK], F32)
        nc.vector.tensor_copy(early_result[:, 0, :], single[0][:])
        nc.scalar.copy(early_result[:, 1, :], single[1][:])
        nc.sync.dma_start(out_view[:, 2:4, tokens(2)], early_result[:])
        quantize_z(LAST)
        late_product(LAST, [0, 1], "bank1", nc.vector.tensor_copy, nc.sync)
        late_product(LAST, [2, 3], "bank2", nc.scalar.copy, nc.scalar)
